import numpy as np, ml_dtypes
CORES = [48,51,52,55]
N = 4
BF = ml_dtypes.bfloat16
def gentries(a):
    return np.ascontiguousarray(a.reshape(8, 16, -1).transpose(0, 2, 1)).reshape(8, -1)
def gtable(e):
    e = np.asarray(e); return np.ascontiguousarray(e.reshape(8, -1, 16).transpose(0, 2, 1)).reshape(128, -1).astype(np.int32)
P, S, C, R = 2048, 64, 128, 4
def members(v):
    return np.stack([gentries(u) for u in v]).reshape(N, 8, R, N, C)
def pack(x, w, a, b):
    return {"fld": x.reshape(N, 128, P).astype(np.float32).astype(BF), "law": w.reshape(N, 128, S * S).astype(np.float32).astype(BF),
            "la": np.stack([gtable(u.reshape(8, -1)) for u in a]), "lb": np.stack([gtable(u.reshape(8, -1)) for u in b])}
def cut(p):
    return p[..., :N * C].reshape(N, 8, R, N, C), p[..., N * C:2 * N * C].reshape(N, 8, R, N, C)
def raw(rng):
    x = rng.integers(-128, 129, (N, 8, 16, P)); x[:, :, 0] = rng.integers(0, S, (N, 8, P))
    w = rng.integers(-16, 17, (N, 8, 16, S * S)); w[:, :, :2] = rng.integers(0, S, (N, 8, 2, S * S))
    a, b = cut(rng.permuted(np.tile(np.arange(P), (N, 8, R, 1)), axis=-1))
    return x, w, a, b
def setup_inputs(rng):
    return pack(*raw(rng))
def setup_inputs_swap(rng):
    x, w, a, b = raw(rng); a2, b2 = a.copy(), b.copy()
    for t in range(R):
        a2[:, :, t], b2[:, :, t] = (a[:, :, 0], b[:, :, 0]) if t % 2 == 0 else (b[:, :, 0], a[:, :, 0])
    return pack(x, w, a2, b2)
def setup_inputs_ends(rng):
    x, w, a, b = raw(rng); x[:, :, 0] = (S - 1) * rng.integers(0, 2, (N, 8, P)); w[:, :, :2] = (S - 1) * rng.integers(0, 2, (N, 8, 2, S * S))
    x[:, :, 1:] = 256 * rng.integers(0, 2, (N, 8, 15, P)) - 128; w[:, :, 2:] = 32 * rng.integers(0, 2, (N, 8, 14, S * S)) - 16
    w[:, :, 2::2] = 32 * rng.integers(0, 2, (N, 8, 7, 1)) - 16
    p = np.concatenate([np.arange(N * C), np.arange(P)[::-1][:N * C]])
    a, b = cut(np.tile(p, (N, 8, R, 1))); return pack(x, w, a, b)
def setup_inputs_one(rng):
    x, w, a, b = raw(rng); x[:, :, 0] = rng.integers(0, S, (N, 8, 1)); return pack(x, w, a, b)
def setup_inputs_spread(rng):
    x, w, a, b = raw(rng)
    x[:, :, 0] = np.floor(S * rng.random((N, 8, P)) ** 3); w[:, :, :2] = np.floor(S * rng.random((N, 8, 2, S * S)) ** 3)
    x[:, :, 1:] = np.floor(np.exp2(7 * rng.random((N, 8, 15, P)))) * rng.choice(np.array([-1, 0, 1]), (N, 8, 15, P))
    w[:, :, 2:] = np.floor(np.exp2(4 * rng.random((N, 8, 14, S * S)))) * rng.choice(np.array([-1, 0, 0, 1]), (N, 8, 14, S * S))
    a, b = cut(np.argsort(rng.random((N, 8, R, P)) + 2 * rng.random((N, 8, 1, P)), axis=-1)); return pack(x, w, a, b)
def check_inputs(d):
    bad = []; x = np.asarray(d["fld"]).astype(np.float32).reshape(N, 8, 16, P); w = np.asarray(d["law"]).astype(np.float32).reshape(N, 8, 16, S * S)
    if not ((x == np.floor(x)).all() and (x[:, :, 0] >= 0).all() and (x[:, :, 0] < S).all() and (np.abs(x[:, :, 1:]) <= 128).all()): bad.append("fields")
    if not ((w == np.floor(w)).all() and (w[:, :, :2] >= 0).all() and (w[:, :, :2] < S).all() and (np.abs(w[:, :, 2:]) <= 16).all()): bad.append("law")
    e = np.sort(np.concatenate([members(d["la"]).reshape(N, 8, R, N * C), members(d["lb"]).reshape(N, 8, R, N * C)], -1), -1)
    if not ((e >= 0).all() and (e < P).all()): bad.append("range")
    if not (e[..., 1:] > e[..., :-1]).all(): bad.append("disjoint")
    return bad
def reference(fld, law, la, lb):
    x = fld.astype(np.float32).astype(np.int64).reshape(N, 8, 16, P); w = law.astype(np.float32).astype(np.int64).reshape(N, 8, 16, S * S)
    a, b = members(la), members(lb)
    for t in range(R):
        for r in range(N):
            for q in range(N):
                for g in range(8):
                    u, v = x[r, g], x[q, g]; i, j = a[r, g, t, q], b[q, g, t, r]
                    col = w[r, g][:, u[0, i] * S + v[0, j]]
                    u[0, i] = col[0]; v[0, j] = col[1]
                    u[2:, i] += col[2:]; v[2:, j] -= col[2:]
    return {"y": x.reshape(N, 128, P).astype(np.float32)}

@@ -1,0 +1,421 @@
+from concourse.bass import DstId, RemoteDMATransfer
+from concourse.mybir import AluOpType as A, ActivationFunctionType as F
+
+N, P, R = 4, 2048, 4
+BF, F32, I32, U16 = "bfloat16", "float32", "int32", "uint16"
+SCRATCH = {
+    "la32": ("sbuf", [128, 128], I32), "lb32": ("sbuf", [128, 128], I32),
+    "LA": ("sbuf", [128, 128], U16), "LB": ("sbuf", [128, 128], U16),
+    "ST": ("sbuf", [128, 6144], BF),
+    "SW": ("sbuf", [128, 5120], BF),
+    "T2": ("sbuf", [128, 4096], BF),
+    "LW": ("sbuf", [128, 4096], BF),
+    "PW": ("sbuf", [128, 2048], BF),
+    "XT": ("sbuf", [128, 4096], BF),
+    "OLD": ("sbuf", [128, 4096], BF), "GS": ("sbuf", [128, 4096], BF), "GP": ("sbuf", [128, 4096], BF),
+    "D": ("sbuf", [128, 2048], BF),
+    "DL": ("sbuf", [128, 16, 128], BF),
+    "RX": ("sbuf", [128, 16, 64], BF),
+    "OFF": ("sbuf", [128, 256], U16), "PTR": ("sbuf", [128, 384], U16),
+    "OUT": ("sbuf", [128, 2048], F32),
+    "RW": ("sbuf", [128, 128], F32), "PK": ("sbuf", [128, 4], I32), "KM": ("sbuf", [128, 4], I32),
+    "VAL": ("sbuf", [128, 144], F32), "COL": ("sbuf", [128, 16], F32), "N0": ("sbuf", [128, 20], F32),
+    "W0": ("sbuf", [128, 144], BF), "W5": ("sbuf", [128, 144], BF), "WP": ("sbuf", [128, 144], BF),
+    "M1": ("sbuf", [128, 128], BF), "MZ": ("sbuf", [128, 128], BF), "M2": ("sbuf", [128, 128], BF), "ID": ("sbuf", [128, 128], BF),
+    "R1": ("dram", [128, 256], BF), "RL": ("dram", [4, 128, 256], BF),
+    "PS": ("psum", [128, 512], F32), "PU": ("psum", [128, 512], F32), "PP": ("psum", [128, 512], F32),
+    "PA": ("psum", [128, 512], F32), "PB": ("psum", [128, 512], F32), "PC": ("psum", [128, 512], F32),
+    "PD": ("psum", [128, 512], F32), "PE": ("psum", [128, 512], F32),
+}
+SEMAPHORES = (["cv", "cs", "cp", "cg", "sent0", "sent", "at2"] + ["ax%d" % t for t in range(R)] + ["ad%d" % t for t in range(R)]
+              + ["m%d" % k for k in range(20)])
+
+PLAN = """
+iota g PK; load y la; fill v 0; load y r1; iota g RW; load y fld; const v 0; const v 1; iota g VAL; const v 2; const v 3;
+double s 0; double s 1; load s lb; mat v W0; fill s 2; const v 4; mat v ID; double v 2; double v 3; xt0 v 1; xt0 s 0;
+rows_out g; narrow v 0; double v 4; fill s 1; const v 5; scatter v 0 0 2; first s 0; narrow v 1; first s 1; const v 7;
+wrap p 0; post s 0 0; post s 0 1; xt g 1; fill g 3; scatter v 0 2 4; pgather s 1 0; mat v WP; lo y 1; load y own;
+pgather v 1 1; start_sw s 0; mat v W5; pwrap p 1; scatter v 1 0 2; mine p 0; exchange g 0; join p 0; offsets v 0;
+const v 8; start_sw s 1; xt g 2; rows_in y; new_v s 0 0; new_v s 0 1; lo y 2; new_u v 0; new_v s 0 3; const v 6;
+load y law; pcast v 1; new_v s 0 2;
+sgather s 1 0 32; sgather v 1 32 64; wrap p 1; post s 1 2; exchange g 1; scatter v 1 2 4; pgather s 2 0; raw s 0 4;
+mine p 1; pgather v 2 1; scatter v 2 0 1; pwrap p 2; join p 1; offsets v 1; new_v s 1 1; pcast v 2; new_v s 1 2;
+mat v M2; new_u v 1; new_v s 1 0; new_v s 1 3;
+sgather s 2 0 32; sgather v 2 32 64; mat v MZ; mat v M1; wrap p 2; post s 2 2; raw s 1 4; scatter v 2 1 2; xt g 3;
+open2 p 0; mine p 2; sum1 p 0; send g 0 0; lo y 3; send g 0 1; close2 p 0 0; keep2 s 0 0; close2 p 0 1; keep2 s 0 1;
+scatter v 2 2 4; pgather v 3 1; close2 p 0 2; close2 p 0 3; exchange g 2; join p 2; send g 1 0; send g 1 1; keep1 s 0;
+offsets v 2; keep2 s 0 3; keep2 s 0 2; ogather s 1 0; pgather s 3 0; pwrap p 3; new_v s 2 1; new_v s 2 0; new_u v 2;
+pcast v 3; new_v s 2 3; new_v s 2 2;
+sgather v 3 48 64; sgather s 3 32 48; ogather s 1 1; raw s 2 4; sgather v 3 0 32; wrap p 3; post v 3 1; open2 p 1;
+close2 p 1 3; exchange g 3; close2 p 1 0; close2 p 1 1; keep2 s 1 0; keep2 s 1 3; scatter v 3 0 2; close2 p 1 2;
+keep2 s 1 2; sum1 p 1; keep2 s 1 1; scatter v 3 2 3; wrap_u p; join p 3; offsets v 3; keep1 s 1; raw v 3 1;
+ogather s 2 0; send g 2 0; sum1 p 2; ogather s 2 1; open2 p 2; raw s 3 0; close2 p 2 3; send g 2 1; close2 p 2 1;
+close2 p 2 0; send g 3 0; raw s 3 2; scatter v 3 3 4; keep1 s 2; keep2 v 2 0; close2 p 2 2; pwrap p 4; keep2 s 2 1;
+keep2 s 2 2; keep2 v 2 3; ogather s 3 0; send g 3 1; raw v 3 3; ogather v 3 1; sum1 p 3; open2 p 3; close2 p 3 3;
+pcast v 4; keep2 v 3 3; close2 p 3 2; keep1 s 3; close2 p 3 0; keep2 s 3 0; keep2 v 3 2; close2 p 3 1; keep2 v 3 1;
+final v 0; final v 2; final s 1; store y 0; final v 4; final s 3; store y 1; final s 5; store y 2
+"""
+ORDER = [tuple(int(w) if w.isdigit() else w for w in x.split()) for x in PLAN.split(";")]
+CUTS = [0, 8, 16, 40, 64, 96, 128]
+
+
+def rank_program(g, core, T, topo):
+    me = T.rank_of(core)
+    if me is None:
+        return
+    Q = {"v": g.vector, "s": g.scalar, "p": g.tensor, "g": g, "y": g.sync}
+    own = {"v": "cv", "s": "cs", "p": "cp", "g": "cg"}
+    total, waited = {}, {}
+    seen = {q: {} for q in Q}
+    writer, readers = {}, {}
+    ndma = [0]
+
+    def need(q, tok):
+        sem, val, known = tok
+        if seen[q].get(sem, 0) < val:
+            Q[q].wait_ge(T.sem[sem], val)
+            waited[sem] = max(waited.get(sem, 0), val)
+            seen[q][sem] = val
+            for k, v in known.items():
+                seen[q][k] = max(seen[q].get(k, 0), v)
+
+    def before(q, rd, wr):
+        toks = [writer[r] for r in rd + wr if r in writer] + [k for r in wr for k in readers.get(r, [])]
+        for tok in sorted(toks, key=lambda k: -k[1]):
+            need(q, tok)
+
+    def after(q, sem, n, rd, wr):
+        total[sem] = total.get(sem, 0) + n
+        tok = (sem, total[sem], dict(seen[q]))
+        for r in rd:
+            readers.setdefault(r, []).append(tok)
+        for r in wr:
+            writer[r] = tok
+            readers[r] = []
+
+    def op(q, rd, wr, call):
+        before(q, rd, wr)
+        call().then_inc(T.sem[own[q]], 1)
+        after(q, own[q], 1, rd, wr)
+
+    def dma(q, rd, wr, out, in_):
+        before(q, rd, wr)
+        sem = "m%d" % ndma[0]
+        ndma[0] += 1
+        Q[q].dma_start(out, in_).then_inc(T.sem[sem], 16)
+        after(q, sem, 16, rd, wr)
+
+    others = [(me + d) % N for d in range(1, N)]
+    ids = {}
+    for q in others:
+        rid, pid = topo.addr(T.cores[q])[:2]
+        ids[q] = DstId(rid=rid, pnc=pid)
+    eng = [e for e in topo.engines(T.cores[0], T.cores[1])
+           if all(e in topo.engines(a, b) for a in T.cores for b in T.cores if a != b)]
+    ne = len(eng)
+
+    def bits(es):
+        return sum(1 << e for e in es)
+
+    def cast(rd, src, dst, arr, res, loc):
+        before("g", rd, [res, loc])
+        g.remote_dma_fused([RemoteDMATransfer(dst_ids=[ids[q] for q in others], dma_engine_mask=bits(eng), remote_sem=T.sem[arr],
+                                              srcs=[src], dsts=[dst] * len(others))], local_sem=T.sem[loc])
+        after("g", loc, ne, [], [loc] if loc != "sent" else [])
+        total[arr] = ne * len(others)
+        writer[res] = (arr, total[arr], {})
+
+    def deal(r):
+        far = sorted([(r + d) % N for d in range(1, N)], key=lambda q: topo.die(T.cores[q]) == topo.die(T.cores[r]))
+        return [[(far[0], eng[:ne // 2]), (far[1], eng[ne // 2:])], [(far[2], eng)]]
+
+    turn = [r for part in deal(me) for r, es in part] + [me]
+
+    def send(q, t, k):
+        part = deal(me)[k]
+        before("g", ["D%d_%d" % (t, turn.index(r)) for r, es in part], ["DL%d" % t])
+        g.remote_dma_fused([RemoteDMATransfer(dst_ids=[ids[r]], dma_engine_mask=bits(es), remote_sem=T.sem["ad%d" % t],
+                                              src=T.D[:, t * 512 + r * 128:t * 512 + r * 128 + 128], dst=T.DL[:, t * 4 + me])
+                            for r, es in part], local_sem=T.sem.sent)
+        after("g", "sent", ne, [], [])
+        if k:
+            total["ad%d" % t] = sum(len(es) for r in others for pt in deal(r) for x, es in pt if x == me)
+            writer["DL%d" % t] = ("ad%d" % t, total["ad%d" % t], {})
+
+    V, S = g.vector, g.scalar
+    KF, E0, NE0, CW5, CWP, CT, CW2 = 0, 1, 6, 8, 9, 10, 11
+
+    def col(k):
+        return T.COL[:, k:k + 1]
+
+    def gather(q, rd, wr, out, win, off, scale=None):
+        if q == "s":
+            if scale is None:
+                op(q, rd, wr, lambda: S.activation(out, win.indirect(off), F.Copy))
+            else:
+                op(q, rd, wr, lambda: S.activation(out, win.indirect(off), F.Copy, scale=scale))
+        elif scale is None:
+            op(q, rd, wr, lambda: V.tensor_copy(out, win.indirect(off)))
+        else:
+            op(q, rd, wr, lambda: V.tensor_scalar(out, win.indirect(off), scale, None, A.mult))
+
+    def copy(q, rd, wr, out, in_, scale=None, bias=None):
+        if q == "s":
+            if bias is not None:
+                op(q, rd, wr, lambda: S.activation(out, in_, F.Identity, bias=bias))
+            elif scale is not None:
+                op(q, rd, wr, lambda: S.activation(out, in_, F.Copy, scale=scale))
+            else:
+                op(q, rd, wr, lambda: S.activation(out, in_, F.Copy))
+        elif bias is not None:
+            op(q, rd, wr, lambda: V.tensor_scalar(out, in_, bias, None, A.add))
+        elif scale is not None:
+            op(q, rd, wr, lambda: V.tensor_scalar(out, in_, scale, None, A.mult))
+        else:
+            op(q, rd, wr, lambda: V.tensor_copy(out, in_))
+
+    def wrap16(rd, bank, n, w, src, a, close=True):
+        before("p", rd + [w], [bank])
+        for s in range(16):
+            ins = g.tensor.matmul(T[bank][:, 0:n], T[w][:, 15 - s:143 - s], T[src][:, a + s:a + 16 * n:16], s == 0, close and s == 15)
+        if close:
+            ins.then_inc(T.sem.cp, 1)
+            after("p", "cp", 1, rd + [w], [bank])
+
+    def lists(t, h, a=0, b=32):
+        return (T.LA, T.LB)[h][:, 32 * t + a:32 * t + b]
+
+    def ptr(t, a, b):
+        return T.PTR[:, 64 * (t - 1) + a:64 * (t - 1) + b]
+
+    def sw_res(t):
+        return ["SW0a", "SW0b"] + ["SW%d_%d" % (k, c) for k in range(t) for c in range(5)]
+
+    def st_res(t):
+        return ["fld"] + ["ST%d_%d" % (k, c) for k in range(t) for c in range(5)]
+
+    fill_res = ["T2f%d" % k for k in range(4)]
+    t2_res = fill_res + ["T2_%d" % k for k in range(5)]
+
+    def load(q, what):
+        if what == "r1":
+            dma(q, [], ["R1"], T.R1[:, :], T.law[1:128:16, :])
+        elif what == "la":
+            dma(q, [], ["la32"], T.la32[:, :], T.la[:, :])
+        elif what == "lb":
+            dma(q, [], ["lb32"], T.lb32[:, :], T.lb[:, :])
+        elif what == "fld":
+            dma(q, [], ["fld"], T.ST[:, 0:P], T.fld[:, :])
+        elif what == "own":
+            dma(q, fill_res, ["T2_4"], T.T2[4:128:16, :], T.law[0:128:16, :])
+            dma(q, fill_res, ["T2_%d" % me], T.T2[me:128:16, :], T.law[1:128:16, :])
+        else:
+            dma(q, ["sent0"], ["LW"], T.LW[:, :], T.law[:, :])
+
+    def iota(q, what):
+        if what == "PK":
+            op(q, [], ["PK"], lambda: g.iota(T.PK[:, 0:1], [[0, 1]], 0, 1))
+        elif what == "RW":
+            op(q, [], ["RW"], lambda: g.iota(T.RW[:, :], [[1, 128]], 0, 0, allow_small_or_imprecise_dtypes=True))
+        else:
+            op(q, [], ["VAL"], lambda: g.iota(T.VAL[:, :], [[-1, 144]], 15, 1, allow_small_or_imprecise_dtypes=True))
+
+    def rows_out(q):
+        cast(["R1"], T.R1[:, :], T.RL[me], "at2", "RL", "sent")
+
+    def rows_in(q):
+        for r in others:
+            dma(q, ["RL"] + fill_res, ["T2_%d" % r], T.T2[r:128:16, :], T.RL[r])
+
+    def start_sw(q, h):
+        copy(q, ["fld", "E"], ["SW0" + "ab"[h]], T.SW[:, 1024 * h:1024 * h + 1024], T.ST[:, 1024 * h:1024 * h + 1024], scale=col(E0))
+
+    def fill(q, k):
+        if q == "g":
+            op(q, [], ["T2f%d" % k], lambda: g.iota(T.T2[:, 1024 * k:1024 * k + 1024], [[0, 1024]], 0, 0, allow_small_or_imprecise_dtypes=True))
+        elif q == "v":
+            before(q, ["T2f0"] if k else [], [])
+            op(q, [], ["T2f%d" % k], lambda: V.memset(T.T2[:, 1024 * k:1024 * k + 1024], 0.0))
+        else:
+            copy(q, ["T2f0"], ["T2f%d" % k], T.T2[:, 1024 * k:1024 * k + 1024], T.T2[:, 0:1024])
+
+    def const(q, k):
+        if k == 0:
+            op(q, ["PK"], ["KM"], lambda: V.tensor_scalar(T.KM[:, 0:1], T.PK[:, 0:1], 15, None, A.bitwise_and))
+        elif k == 1:
+            copy(q, ["KM"], ["KF"], col(KF), T.KM[:, 0:1])
+        elif k == 2:
+            op(q, ["RW", "KF"], ["E"], lambda: V.tensor_scalar(T.COL[:, E0:E0 + 5], T.RW[:, 0:5], col(KF), None, A.is_equal))
+        elif k == 3:
+            copy(q, ["RW", "E"], ["N0"], T.N0[:, 0:17], T.RW[:, 0:17], scale=col(E0))
+        elif k == 4:
+            op(q, ["KF"], ["CW5"], lambda: V.tensor_scalar(col(CW5), col(KF), 5.0, None, A.is_lt))
+        elif k == 5:
+            op(q, ["E"], ["CWP"], lambda: V.tensor_scalar(col(CWP), col(E0), 128.0, col(E0 + 1), A.mult, A.add))
+        elif k == 6:
+            op(q, ["RW", "KF"], ["NE"], lambda: V.tensor_scalar(T.COL[:, NE0:NE0 + 2], T.RW[:, 0:2], col(KF), None, A.not_equal))
+        elif k == 7:
+            op(q, ["E"], ["CT"], lambda: V.tensor_scalar(col(CT), col(E0 + 1), 2.0, col(E0), A.mult, A.add))
+        else:
+            op(q, ["CT"], ["CW2"], lambda: V.tensor_scalar(col(CW2), col(CT), -1.0, None, A.add))
+
+    def mat(q, name):
+        rd, a, b, s1, s2 = {"W0": (["KF", "E"], 0, 144, col(KF), col(E0)), "W5": (["KF", "CW5"], 0, 144, col(KF), col(CW5)),
+                            "WP": (["KF", "CWP"], 0, 144, col(KF), col(CWP)), "M1": (["NE"], 15, 143, 0.0, col(NE0 + 1)),
+                            "MZ": (["NE"], 15, 143, 0.0, col(NE0)), "M2": (["E", "CW2"], 15, 143, col(E0 + 1), col(CW2)),
+                            "ID": ([], 15, 143, 0.0, 1.0)}[name]
+        op(q, ["VAL"] + rd, [name], lambda: V.tensor_scalar(T[name][:, 0:b - a], T.VAL[:, a:b], s1, s2, A.is_equal, A.mult))
+
+    def double(q, k):
+        if k == 0:
+            copy(q, ["RW", "E"], ["PW"], T.PW[:, 0:128], T.RW[:, :], scale=col(E0 + 1))
+        else:
+            n = 64 << k
+            copy(q, ["N0", "PW"], ["PW" if k < 4 else "PWb"], T.PW[:, n:2 * n], T.PW[:, 0:n], bias=T.N0[:, n >> 7:(n >> 7) + 1])
+
+    def xt0(q, h):
+        copy(q, ["PW", "N0"], ["XT0_%d" % h], T.XT[:, 512 * h:512 * h + 512], T.PW[:, 512 * h:512 * h + 512], bias=T.N0[:, 16:17])
+
+    def xt(q, t):
+        op(q, [], ["XT%d_0" % t, "XT%d_1" % t],
+           lambda: g.iota(T.XT[:, t * 1024:t * 1024 + 1024], [[1, 8], [0, 128]], 16 + 8 * t, 0, allow_small_or_imprecise_dtypes=True))
+
+    def lo(q, t):
+        dma(q, ["XT0_0", "XT0_1"], ["XT%d_0" % t, "XT%d_1" % t], T.XT[1:128:16, t * 1024:t * 1024 + 1024], T.XT[1:128:16, 0:1024])
+
+    def narrow(q, h):
+        copy(q, [("la32", "lb32")[h]], ["L%d" % h], (T.LA, T.LB)[h][:, :], (T.la32, T.lb32)[h][:, :])
+
+    def scatter(q, t, a, b):
+        h = a // 2
+        op(q, ["XT%d_%d" % (t, h), "L%d" % h], ["PW", "PWb"],
+           lambda: V.tensor_copy(T.PW[:, :].indirect(lists(t, h, 16 * a - 32 * h, 16 * b - 32 * h)), T.XT[:, t * 1024 + 256 * a:t * 1024 + 256 * b]))
+
+    def pgather(q, t, h):
+        gather(q, ["PW", "L%d" % h], ["GP%d_%d" % (t, h)], T.GP[:, t * 1024 + h * 512:t * 1024 + h * 512 + 512], T.PW[:, :], lists(t, h))
+
+    def pwrap(q, t):
+        if t < R:
+            wrap16(["GP%d_0" % t, "GP%d_1" % t], "PP", 64, "WP", "GP", t * 1024)
+        else:
+            wrap16(["PW"], "PP", 128, "WP", "PW", 0)
+
+    def pcast(q, t):
+        n = 64 if t < R else 128
+        copy(q, [], ["PP", "PTR%d" % t], ptr(t, 0, n), T.PP[:, 0:n])
+
+    def first(q, h):
+        gather(q, ["fld", "L%d" % h], ["OLD0_%d" % h], T.OLD[:, 512 * h:512 * h + 512], T.ST[:, 0:P], lists(0, h))
+
+    def sgather(q, t, a, b):
+        gather(q, sw_res(t) + ["PTR%d" % t], ["GS%d_%d" % (t, a)], T.GS[:, t * 1024 + 16 * a:t * 1024 + 16 * b], T.SW[:, 0:P + 1024 * t],
+               ptr(t, a, b), 64.0 if a < 32 else None)
+
+    def wrap(q, t):
+        if t == 0:
+            wrap16(["OLD0_0", "OLD0_1"], "PS", 64, "W0", "OLD", 0)
+        elif t < R - 1:
+            wrap16(["GS%d_0" % t, "GS%d_32" % t], "PS", 64, "W5", "GS", t * 1024)
+        else:
+            wrap16(["GS3_32", "GS3_48"], "PS", 32, "W5", "GS", t * 1024 + 512)
+
+    def wrap_u(q):
+        wrap16(["GS3_0"], "PU", 32, "W5", "GS", 3 * 1024, False)
+
+    def post(q, t, h):
+        if h == 2:
+            copy(q, [], ["PS", "RXu%d" % t, "RXv%d" % t], T.RX[:, t * 4 + me, :], T.PS[:, 0:64])
+        elif t == 0:
+            copy(q, [], ["PS", "RX%s0" % "uv"[h]], T.RX[:, me, 32 * h:32 * h + 32], T.PS[:, 32 * h:32 * h + 32], scale=None if h else 64.0)
+        else:
+            copy(q, [], ["PS", "RXv3"], T.RX[:, 12 + me, 32:64], T.PS[:, 0:32])
+
+    def exchange(q, t):
+        a = 0 if t < R - 1 else 32
+        cast(["RXu%d" % t, "RXv%d" % t][a // 32:], T.RX[:, t * 4 + me, a:64], T.RX[:, t * 4 + me, a:64], "ax%d" % t, "AX%d" % t, "sent0" if t == 0 else "sent")
+
+    def mine(q, t):
+        before(q, ["RXu%d" % t, "RXv%d" % t, "ID"], ["PU"])
+        g.tensor.matmul(T.PU[:, 0:64], T.ID[:, :], T.RX[:, t * 4 + me, :], True, False)
+
+    def join(q, t):
+        halves = 2 if t < R - 1 else 1
+        rd = ["AX%d" % t, "RXv%d" % t, "ID"]
+        before(q, rd, ["open"])
+        for h in range(halves):
+            a = 32 * (1 - h) + 8 * me
+            ins = g.tensor.matmul(T.PU[:, 32 * h:32 * h + 32], T.ID[:, :], T.RX[:, t * 4:t * 4 + 4, a:a + 8], False, h == halves - 1)
+        ins.then_inc(T.sem.cp, 1)
+        after(q, "cp", 1, rd, ["PU"])
+
+    def offsets(q, t):
+        n = 64 if t < R - 1 else 32
+        copy(q, [], ["PU", "OFF%d" % t], T.OFF[:, t * 64:t * 64 + n], T.PU[:, 0:n])
+
+    def new_u(q, t):
+        b = P + 1024 * t
+        gather(q, t2_res + ["OFF%d" % t, "E"], ["SW%d_4" % t], T.SW[:, b:b + 512], T.T2[:, :], T.OFF[:, t * 64:t * 64 + 32], col(E0 + 4))
+
+    def new_v(q, t, c):
+        b = P + 1024 * t + 512 + 128 * c
+        gather(q, t2_res + ["OFF%d" % t, "E"], ["SW%d_%d" % (t, c)], T.SW[:, b:b + 128], T.T2[:, :],
+               T.OFF[:, t * 64 + 32 + 8 * c:t * 64 + 40 + 8 * c], col(E0 + c))
+
+    def raw(q, t, k):
+        a, b = (0, 4) if k == 4 else (turn[k], turn[k] + 1)
+        gather(q, ["LW", "OFF%d" % t], ["D%d_%d" % (t, turn.index(c)) for c in range(a, b)], T.D[:, t * 512 + 128 * a:t * 512 + 128 * b], T.LW[:, :],
+               T.OFF[:, t * 64 + 8 * a:t * 64 + 8 * b])
+
+    def ogather(q, t, h):
+        gather(q, st_res(t) + ["PTR%d" % t], ["OLD%d_%d" % (t, h)], T.OLD[:, t * 1024 + h * 512:t * 1024 + h * 512 + 512],
+               T.ST[:, 0:P + 1024 * t], ptr(t, 32 * h, 32 * h + 32))
+
+    def sum1(q, t):
+        rd = ["D%d_%d" % (t, c) for c in range(N)] + ["OLD%d_0" % t, "M1", "MZ"]
+        before(q, rd, ["PA"])
+        g.tensor.matmul(T.PA[:, :], T.MZ[:, :], T.OLD[:, t * 1024:t * 1024 + 512], True, False)
+        g.tensor.matmul(T.PA[:, :], T.M1[:, :], T.D[:, t * 512:t * 512 + 512], False, True).then_inc(T.sem.cp, 1)
+        after(q, "cp", 1, rd, ["PA"])
+
+    banks = ["PB", "PC", "PD", "PE"]
+
+    def open2(q, t):
+        before(q, ["OLD%d_1" % t, "MZ"], banks)
+        for k in range(N):
+            a = t * 1024 + 512 + 128 * turn[k]
+            g.tensor.matmul(T[banks[k]][:, 0:128], T.MZ[:, :], T.OLD[:, a:a + 128], True, False)
+
+    def close2(q, t, k):
+        c = turn[k]
+        rd = ["D%d_3" % t if c == me else "DL%d" % t, "M2"]
+        before(q, rd, ["open%d" % k])
+        d = T.D[:, t * 512 + 128 * c:t * 512 + 128 * c + 128] if c == me else T.DL[:, t * 4 + c]
+        g.tensor.matmul(T[banks[k]][:, 0:128], T.M2[:, :], d, False, True).then_inc(T.sem.cp, 1)
+        after(q, "cp", 1, rd, [banks[k]])
+
+    def keep1(q, t):
+        copy(q, [], ["PA", "ST%d_0" % t], T.ST[:, P + 1024 * t:P + 1024 * t + 512], T.PA[:, :])
+
+    def keep2(q, t, k):
+        b = P + 1024 * t + 512 + 128 * turn[k]
+        copy(q, [], [banks[k], "ST%d_%d" % (t, k + 1)], T.ST[:, b:b + 128], T[banks[k]][:, 0:128])
+
+    def final(q, k):
+        a, b = CUTS[k], CUTS[k + 1]
+        gather(q, st_res(R) + ["PTR4"], ["OUT%d" % k], T.OUT[:, 16 * a:16 * b], T.ST[:, :], ptr(R, a, b))
+
+    def store(q, k):
+        a, b = 16 * CUTS[2 * k], 16 * CUTS[2 * k + 2]
+        dma(q, ["OUT%d" % (2 * k), "OUT%d" % (2 * k + 1)], ["y%d" % k], T.y[:, a:b], T.OUT[:, a:b])
+
+    steps = {"load": load, "iota": iota, "rows_out": rows_out, "rows_in": rows_in, "start_sw": start_sw, "fill": fill, "const": const,
+             "mat": mat, "double": double, "xt0": xt0, "xt": xt, "lo": lo, "narrow": narrow, "scatter": scatter, "pgather": pgather,
+             "pwrap": pwrap, "pcast": pcast, "first": first, "sgather": sgather, "wrap": wrap, "wrap_u": wrap_u, "post": post,
+             "exchange": exchange, "mine": mine, "join": join, "offsets": offsets, "new_u": new_u, "new_v": new_v, "raw": raw,
+             "send": send, "ogather": ogather, "sum1": sum1, "open2": open2, "close2": close2, "keep1": keep1, "keep2": keep2,
+             "final": final, "store": store}
+    for task in ORDER:
+        steps[task[0]](*task[1:])
+    for sem in sorted(total):
+        if waited.get(sem, 0) < total[sem]:
+            g.wait_ge(T.sem[sem], total[sem])

@@ -6,8 +6,9 @@ BF, F32, I32, U16 = "bfloat16", "float32", "int32", "uint16"
 SCRATCH = {
     "la32": ("sbuf", [128, 128], I32), "lb32": ("sbuf", [128, 128], I32),
     "LA": ("sbuf", [128, 128], U16), "LB": ("sbuf", [128, 128], U16),
-    "ST": ("sbuf", [128, 6144], BF),
-    "SW": ("sbuf", [128, 5120], BF),
+    "FD": ("sbuf", [128, 2048], BF),
+    "EW": ("sbuf", [128, 4112], BF),
+    "SW": ("sbuf", [128, 3088], BF),
     "T2": ("sbuf", [128, 4096], BF),
     "LW": ("sbuf", [128, 4096], BF),
     "PW": ("sbuf", [128, 2048], BF),
@@ -19,44 +20,40 @@ SCRATCH = {
     "OFF": ("sbuf", [128, 256], U16), "PTR": ("sbuf", [128, 384], U16),
     "OUT": ("sbuf", [128, 2048], F32),
     "RW": ("sbuf", [128, 128], F32), "PK": ("sbuf", [128, 4], I32), "KM": ("sbuf", [128, 4], I32),
-    "VAL": ("sbuf", [128, 144], F32), "COL": ("sbuf", [128, 16], F32), "N0": ("sbuf", [128, 20], F32),
-    "W0": ("sbuf", [128, 144], BF), "W5": ("sbuf", [128, 144], BF), "WP": ("sbuf", [128, 144], BF),
+    "VAL": ("sbuf", [128, 144], F32), "COL": ("sbuf", [128, 16], F32), "N0": ("sbuf", [128, 8], F32),
+    "W0": ("sbuf", [128, 144], BF), "WA": ("sbuf", [128, 144], BF), "WP": ("sbuf", [128, 144], BF),
     "M1": ("sbuf", [128, 128], BF), "MZ": ("sbuf", [128, 128], BF), "M2": ("sbuf", [128, 128], BF), "ID": ("sbuf", [128, 128], BF),
     "R1": ("dram", [128, 256], BF), "RL": ("dram", [4, 128, 256], BF),
-    "PS": ("psum", [128, 512], F32), "PU": ("psum", [128, 512], F32), "PP": ("psum", [128, 512], F32),
-    "PA": ("psum", [128, 512], F32), "PB": ("psum", [128, 512], F32), "PC": ("psum", [128, 512], F32),
-    "PD": ("psum", [128, 512], F32), "PE": ("psum", [128, 512], F32),
+    "PS0": ("psum", [128, 512], F32), "PS1": ("psum", [128, 512], F32), "PU": ("psum", [128, 512], F32), "PP": ("psum", [128, 512], F32),
+    "PA": ("psum", [128, 512], F32), "PB": ("psum", [128, 512], F32), "PC": ("psum", [128, 512], F32), "PD": ("psum", [128, 512], F32),
 }
 SEMAPHORES = (["cv", "cs", "cp", "cg", "sent0", "sent", "at2"] + ["ax%d" % t for t in range(R)] + ["ad%d" % t for t in range(R)]
-              + ["m%d" % k for k in range(20)])
+              + ["m%d" % k for k in range(36)])
 
 PLAN = """
-iota g PK; load y la; fill v 0; load y r1; iota g RW; load y fld; const v 0; const v 1; iota g VAL; const v 2; const v 3;
-double s 0; double s 1; load s lb; mat v W0; fill s 2; const v 4; mat v ID; double v 2; double v 3; xt0 v 1; xt0 s 0;
-rows_out g; narrow v 0; double v 4; fill s 1; const v 5; scatter v 0 0 2; first s 0; narrow v 1; first s 1; const v 7;
-wrap p 0; post s 0 0; post s 0 1; xt g 1; fill g 3; scatter v 0 2 4; pgather s 1 0; mat v WP; lo y 1; load y own;
-pgather v 1 1; start_sw s 0; mat v W5; pwrap p 1; scatter v 1 0 2; mine p 0; exchange g 0; join p 0; offsets v 0;
-const v 8; start_sw s 1; xt g 2; rows_in y; new_v s 0 0; new_v s 0 1; lo y 2; new_u v 0; new_v s 0 3; const v 6;
-load y law; pcast v 1; new_v s 0 2;
-sgather s 1 0 32; sgather v 1 32 64; wrap p 1; post s 1 2; exchange g 1; scatter v 1 2 4; pgather s 2 0; raw s 0 4;
-mine p 1; pgather v 2 1; scatter v 2 0 1; pwrap p 2; join p 1; offsets v 1; new_v s 1 1; pcast v 2; new_v s 1 2;
-mat v M2; new_u v 1; new_v s 1 0; new_v s 1 3;
-sgather s 2 0 32; sgather v 2 32 64; mat v MZ; mat v M1; wrap p 2; post s 2 2; raw s 1 4; scatter v 2 1 2; xt g 3;
-open2 p 0; mine p 2; sum1 p 0; send g 0 0; lo y 3; send g 0 1; close2 p 0 0; keep2 s 0 0; close2 p 0 1; keep2 s 0 1;
-scatter v 2 2 4; pgather v 3 1; close2 p 0 2; close2 p 0 3; exchange g 2; join p 2; send g 1 0; send g 1 1; keep1 s 0;
-offsets v 2; keep2 s 0 3; keep2 s 0 2; ogather s 1 0; pgather s 3 0; pwrap p 3; new_v s 2 1; new_v s 2 0; new_u v 2;
-pcast v 3; new_v s 2 3; new_v s 2 2;
-sgather v 3 48 64; sgather s 3 32 48; ogather s 1 1; raw s 2 4; sgather v 3 0 32; wrap p 3; post v 3 1; open2 p 1;
-close2 p 1 3; exchange g 3; close2 p 1 0; close2 p 1 1; keep2 s 1 0; keep2 s 1 3; scatter v 3 0 2; close2 p 1 2;
-keep2 s 1 2; sum1 p 1; keep2 s 1 1; scatter v 3 2 3; wrap_u p; join p 3; offsets v 3; keep1 s 1; raw v 3 1;
-ogather s 2 0; send g 2 0; sum1 p 2; ogather s 2 1; open2 p 2; raw s 3 0; close2 p 2 3; send g 2 1; close2 p 2 1;
-close2 p 2 0; send g 3 0; raw s 3 2; scatter v 3 3 4; keep1 s 2; keep2 v 2 0; close2 p 2 2; pwrap p 4; keep2 s 2 1;
-keep2 s 2 2; keep2 v 2 3; ogather s 3 0; send g 3 1; raw v 3 3; ogather v 3 1; sum1 p 3; open2 p 3; close2 p 3 3;
-pcast v 4; keep2 v 3 3; close2 p 3 2; keep1 s 3; close2 p 3 0; keep2 s 3 0; keep2 v 3 2; close2 p 3 1; keep2 v 3 1;
-final v 0; final v 2; final s 1; store y 0; final v 4; final s 3; store y 1; final s 5; store y 2
+load y r1; load y la; load y lb; iota g PK; iota g RW; iota g VAL; fill v 0 4; fill s 4 8; fill s 8 16; fill y 16 24; zero v; species y PW;
+const v KF; const v E; double v 0; const s N0; double s 1; double s 2; mat v WA; mat v ID; const s CWP; mat s W0; const s NE; mat s WP; const s C64;
+narrow v 0; narrow v 1; const v EW; species y T2; first s 1; first s 0; wrap p 0; post s 0; mine p 0; fill y 24 32; own y 16; double v 3;
+scatter v 0 0 4; pgather v 1 1; const v SW; rows_out g; xt g 1 0; exchange g 0; xt g 1 1; rows_in y; lo y 1 0; lo y 1 1; join p 0;
+offsets v 0; new_u v 0; const s CW2; mat s MZ; mat s M1; pgather s 1 0; pwrap p 1; pcast v 1; new_v s 0;
+
+law y 0 2 sent0; law y 2 4; xt g 2 0; xt g 2 1; lo y 2 0; lo y 2 1; sgather s 1 0 32; sgather s 1 32 64; prewrap p 1; wrap p 1; post s 1; exchange g 1;
+scatter v 1 0 2; mat v M2; scatter v 1 2 4; open2 p 0; mine p 1; raw s 0 4; send g 0 0; send g 0 1; xt g 3 0; xt g 3 1; lo y 3 0; lo y 3 1;
+pgather v 2 1; pgather s 2 0; join p 1; offsets v 1; pwrap p 2; raw v 1 4; new_v s 1; mask_u v 1; pcast v 2; send g 1 0; send g 1 1;
+
+sgather s 2 0 32; sgather s 2 32 64; prewrap p 2; close2 p 0; wrap p 2; keep2 s 0 0; keep2 s 0 1; post s 2; exchange g 2; mine p 2;
+scatter v 2 0 4; ogather s 1 1; ogather s 1 0; open2 p 1; close2 p 1; load y fld AX2;
+pgather v 3 0; pgather s 3 1; join p 2; offsets v 2; pwrap p 3; raw v 2 4; new_v s 2; pcast v 3; mask_u v 2; send g 2 0; send g 2 1; keep2 s 1 0;
+
+sgather v 3 48 64; sgather s 3 32 48; sum1 p 1; prewrap p 3; wrap p 3; sgather s 3 0 32; keep2 s 1 1; post s 3; exchange g 3; wrap_u p;
+scatter v 3 0 4; unreacted y; keep1 s 1; ogather s 2 0; ogather s 2 1; sum1 p 2; keep1 s 2; join p 3; offsets v 3;
+
+raw v 3 0; raw s 3 1; send g 3 0; open2 p 2; close2 p 2; keep2 s 2 1; keep2 v 2 0; raw v 3 2; send g 3 1; pwrap p 4; raw s 3 3;
+ogather v 3 0; ogather s 3 1; sum1 p 3; open2 p 3; keep1 s 3; pcast v 4; close2 p 3; keep2 v 3 0; keep2 s 3 1;
+final v 0; last s 3 0; store y 0 1; last p 3 1; final v 1; store y 1 2; last s 4 0; last p 4 1; last s 3 2; final v 2; store y 2 4; last s 4 2; store y 4 5
 """
 ORDER = [tuple(int(w) if w.isdigit() else w for w in x.split()) for x in PLAN.split(";")]
-CUTS = [0, 8, 16, 40, 64, 96, 128]
+CUTS = [0, 16, 40, 72, 96, 128]
 
 
 def rank_program(g, core, T, topo):
@@ -64,7 +61,7 @@ def rank_program(g, core, T, topo):
     if me is None:
         return
     Q = {"v": g.vector, "s": g.scalar, "p": g.tensor, "g": g, "y": g.sync}
-    own = {"v": "cv", "s": "cs", "p": "cp", "g": "cg"}
+    own_sem = {"v": "cv", "s": "cs", "p": "cp", "g": "cg"}
     total, waited = {}, {}
     seen = {q: {} for q in Q}
     writer, readers = {}, {}
@@ -95,8 +92,8 @@ def rank_program(g, core, T, topo):
 
     def op(q, rd, wr, call):
         before(q, rd, wr)
-        call().then_inc(T.sem[own[q]], 1)
-        after(q, own[q], 1, rd, wr)
+        call().then_inc(T.sem[own_sem[q]], 1)
+        after(q, own_sem[q], 1, rd, wr)
 
     def dma(q, rd, wr, out, in_):
         before(q, rd, wr)
@@ -131,11 +128,14 @@ def rank_program(g, core, T, topo):
 
     turn = [r for part in deal(me) for r, es in part] + [me]
 
+    def dcol(t, a, b):
+        return T.D[:, t * 512 + 128 * a:t * 512 + 128 * b] if t else T.EW[:, 16 + 128 * a:16 + 128 * b]
+
     def send(q, t, k):
         part = deal(me)[k]
         before("g", ["D%d_%d" % (t, turn.index(r)) for r, es in part], ["DL%d" % t])
         g.remote_dma_fused([RemoteDMATransfer(dst_ids=[ids[r]], dma_engine_mask=bits(es), remote_sem=T.sem["ad%d" % t],
-                                              src=T.D[:, t * 512 + r * 128:t * 512 + r * 128 + 128], dst=T.DL[:, t * 4 + me])
+                                              src=dcol(t, r, r + 1), dst=T.DL[:, t * 4 + me])
                             for r, es in part], local_sem=T.sem.sent)
         after("g", "sent", ne, [], [])
         if k:
@@ -143,7 +143,7 @@ def rank_program(g, core, T, topo):
             writer["DL%d" % t] = ("ad%d" % t, total["ad%d" % t], {})
 
     V, S = g.vector, g.scalar
-    KF, E0, NE0, CW5, CWP, CT, CW2 = 0, 1, 6, 8, 9, 10, 11
+    KF, E0, NE0, C64, CWP, CW2 = 0, 1, 6, 8, 9, 10
 
     def col(k):
         return T.COL[:, k:k + 1]
@@ -162,11 +162,13 @@ def rank_program(g, core, T, topo):
     def copy(q, rd, wr, out, in_, scale=None, bias=None):
         if q == "s":
             if bias is not None:
-                op(q, rd, wr, lambda: S.activation(out, in_, F.Identity, bias=bias))
+                op(q, rd, wr, lambda: S.activation(out, in_, F.Identity, bias=bias, scale=1.0 if scale is None else scale))
             elif scale is not None:
                 op(q, rd, wr, lambda: S.activation(out, in_, F.Copy, scale=scale))
             else:
                 op(q, rd, wr, lambda: S.activation(out, in_, F.Copy))
+        elif bias is not None and scale is not None:
+            op(q, rd, wr, lambda: V.tensor_scalar(out, in_, scale, bias, A.mult, A.add))
         elif bias is not None:
             op(q, rd, wr, lambda: V.tensor_scalar(out, in_, bias, None, A.add))
         elif scale is not None:
@@ -174,11 +176,11 @@ def rank_program(g, core, T, topo):
         else:
             op(q, rd, wr, lambda: V.tensor_copy(out, in_))
 
-    def wrap16(rd, bank, n, w, src, a, close=True):
-        before("p", rd + [w], [bank])
+    def wrap16(rd, bank, n, w, src, a, start=True, stop=True):
+        before("p", rd + [w], [bank] if start else [])
         for s in range(16):
-            ins = g.tensor.matmul(T[bank][:, 0:n], T[w][:, 15 - s:143 - s], T[src][:, a + s:a + 16 * n:16], s == 0, close and s == 15)
-        if close:
+            ins = g.tensor.matmul(T[bank][:, 0:n], T[w][:, 15 - s:143 - s], T[src][:, a + s:a + 16 * n:16], start and s == 0, stop and s == 15)
+        if stop:
             ins.then_inc(T.sem.cp, 1)
             after("p", "cp", 1, rd + [w], [bank])
 
@@ -189,28 +191,40 @@ def rank_program(g, core, T, topo):
         return T.PTR[:, 64 * (t - 1) + a:64 * (t - 1) + b]
 
     def sw_res(t):
-        return ["SW0a", "SW0b"] + ["SW%d_%d" % (k, c) for k in range(t) for c in range(5)]
+        return ["SW"] + ["SW%d_%d" % (k, c) for k in range(t) for c in range(5)]
 
-    def st_res(t):
-        return ["fld"] + ["ST%d_%d" % (k, c) for k in range(t) for c in range(5)]
+    def ew_res(t):
+        return ["EW"] + ["D0_%d" % c for c in range(N)] + ["EW%d_%d" % (k, c) for k in range(t) for c in range(3)]
 
-    fill_res = ["T2f%d" % k for k in range(4)]
+    fill_res = ["T2f%d" % k for k in range(32)]
     t2_res = fill_res + ["T2_%d" % k for k in range(5)]
+    row = dict([(me, 1)] + [(r, 2 + k) for k, r in enumerate(others)])
+    lw_res = ["LW%d" % k for k in range(4)]
 
-    def load(q, what):
+    def load(q, what, gate=None):
+        before(q, [gate] if gate else [], [])
         if what == "r1":
             dma(q, [], ["R1"], T.R1[:, :], T.law[1:128:16, :])
         elif what == "la":
             dma(q, [], ["la32"], T.la32[:, :], T.la[:, :])
         elif what == "lb":
             dma(q, [], ["lb32"], T.lb32[:, :], T.lb[:, :])
-        elif what == "fld":
-            dma(q, [], ["fld"], T.ST[:, 0:P], T.fld[:, :])
-        elif what == "own":
-            dma(q, fill_res, ["T2_4"], T.T2[4:128:16, :], T.law[0:128:16, :])
-            dma(q, fill_res, ["T2_%d" % me], T.T2[me:128:16, :], T.law[1:128:16, :])
         else:
-            dma(q, ["sent0"], ["LW"], T.LW[:, :], T.law[:, :])
+            dma(q, [], ["fld"], T.FD[:, :], T.fld[:, :])
+
+    def own(q, a):
+        for r in range(2):
+            dma(q, fill_res[:a], ["T2_%d" % r], T.T2[r:128:16, 0:128 * a], T.law[r:128:16, 0:128 * a])
+
+    def law(q, a, b, gate=None):
+        before(q, [gate] if gate else [], [])
+        dma(q, [], lw_res[a:b], T.LW[:, 1024 * a:1024 * b], T.law[:, 1024 * a:1024 * b])
+
+    def species(q, where):
+        if where == "PW":
+            dma(q, [], ["PW"], T.PW[0:128:16, :], T.fld[0:128:16, :])
+        else:
+            dma(q, fill_res[:16], ["T2_0"], T.T2[0:128:16, 0:P], T.fld[0:128:16, :])
 
     def iota(q, what):
         if what == "PK":
@@ -225,74 +239,89 @@ def rank_program(g, core, T, topo):
 
     def rows_in(q):
         for r in others:
-            dma(q, ["RL"] + fill_res, ["T2_%d" % r], T.T2[r:128:16, :], T.RL[r])
+            dma(q, ["RL"] + fill_res, ["T2_%d" % row[r]], T.T2[row[r]:128:16, :], T.RL[r])
 
-    def start_sw(q, h):
-        copy(q, ["fld", "E"], ["SW0" + "ab"[h]], T.SW[:, 1024 * h:1024 * h + 1024], T.ST[:, 1024 * h:1024 * h + 1024], scale=col(E0))
-
-    def fill(q, k):
+    def fill(q, a, b):
+        out = T.T2[:, 128 * a:128 * b]
         if q == "g":
-            op(q, [], ["T2f%d" % k], lambda: g.iota(T.T2[:, 1024 * k:1024 * k + 1024], [[0, 1024]], 0, 0, allow_small_or_imprecise_dtypes=True))
+            op(q, [], fill_res[a:b], lambda: g.iota(out, [[0, 128 * (b - a)]], 0, 0, allow_small_or_imprecise_dtypes=True))
         elif q == "v":
-            before(q, ["T2f0"] if k else [], [])
-            op(q, [], ["T2f%d" % k], lambda: V.memset(T.T2[:, 1024 * k:1024 * k + 1024], 0.0))
+            op(q, [], fill_res[a:b], lambda: V.memset(out, 0.0))
+        elif q == "y":
+            dma(q, [], fill_res[a:b], out, T.law[:, 128 * a:128 * b])
         else:
-            copy(q, ["T2f0"], ["T2f%d" % k], T.T2[:, 1024 * k:1024 * k + 1024], T.T2[:, 0:1024])
+            copy(q, fill_res[:b - a], fill_res[a:b], out, T.T2[:, 0:128 * (b - a)])
 
     def const(q, k):
-        if k == 0:
+        if k == "KF":
             op(q, ["PK"], ["KM"], lambda: V.tensor_scalar(T.KM[:, 0:1], T.PK[:, 0:1], 15, None, A.bitwise_and))
-        elif k == 1:
             copy(q, ["KM"], ["KF"], col(KF), T.KM[:, 0:1])
-        elif k == 2:
+        elif k == "E":
             op(q, ["RW", "KF"], ["E"], lambda: V.tensor_scalar(T.COL[:, E0:E0 + 5], T.RW[:, 0:5], col(KF), None, A.is_equal))
-        elif k == 3:
-            copy(q, ["RW", "E"], ["N0"], T.N0[:, 0:17], T.RW[:, 0:17], scale=col(E0))
-        elif k == 4:
-            op(q, ["KF"], ["CW5"], lambda: V.tensor_scalar(col(CW5), col(KF), 5.0, None, A.is_lt))
-        elif k == 5:
-            op(q, ["E"], ["CWP"], lambda: V.tensor_scalar(col(CWP), col(E0), 128.0, col(E0 + 1), A.mult, A.add))
-        elif k == 6:
-            op(q, ["RW", "KF"], ["NE"], lambda: V.tensor_scalar(T.COL[:, NE0:NE0 + 2], T.RW[:, 0:2], col(KF), None, A.not_equal))
-        elif k == 7:
-            op(q, ["E"], ["CT"], lambda: V.tensor_scalar(col(CT), col(E0 + 1), 2.0, col(E0), A.mult, A.add))
+        elif k == "N0":
+            copy(q, ["RW", "E"], [k], T.N0[:, :], T.RW[:, 0:8], col(E0 + 1))
+        elif k == "C64":
+            copy(q, ["E"], [k], col(C64), col(E0), 63.0, 1.0)
+        elif k == "CWP":
+            copy(q, ["E"], [k], col(CWP), col(E0 + 1), 128.0, col(E0 + 2))
+        elif k == "NE":
+            copy(q, ["E"], [k], T.COL[:, NE0:NE0 + 2], T.COL[:, E0:E0 + 2], -1.0, 1.0)
+        elif k == "CW2":
+            copy(q, ["E", "NE"], [k], col(CW2), col(NE0), -0.5, col(E0 + 1))
         else:
-            op(q, ["CT"], ["CW2"], lambda: V.tensor_scalar(col(CW2), col(CT), -1.0, None, A.add))
+            op(q, [], [k], lambda: V.memset(T[k][:, 0:16], 0.0))
 
     def mat(q, name):
-        rd, a, b, s1, s2 = {"W0": (["KF", "E"], 0, 144, col(KF), col(E0)), "W5": (["KF", "CW5"], 0, 144, col(KF), col(CW5)),
-                            "WP": (["KF", "CWP"], 0, 144, col(KF), col(CWP)), "M1": (["NE"], 15, 143, 0.0, col(NE0 + 1)),
-                            "MZ": (["NE"], 15, 143, 0.0, col(NE0)), "M2": (["E", "CW2"], 15, 143, col(E0 + 1), col(CW2)),
-                            "ID": ([], 15, 143, 0.0, 1.0)}[name]
-        op(q, ["VAL"] + rd, [name], lambda: V.tensor_scalar(T[name][:, 0:b - a], T.VAL[:, a:b], s1, s2, A.is_equal, A.mult))
+        if name == "WA":
+            op(q, ["VAL", "KF"], [name], lambda: V.tensor_scalar(T.WA[:, :], T.VAL[:, :], col(KF), None, A.is_equal))
+        elif name == "ID":
+            op(q, ["VAL"], [name], lambda: V.tensor_scalar(T.ID[:, :], T.VAL[:, 15:143], 0.0, None, A.is_equal))
+        elif name == "M2":
+            copy(q, ["CW2"], ["CW2"], col(CW2), col(CW2), 2.0)
+            op(q, ["VAL", "E", "CW2"], [name], lambda: V.tensor_scalar(T.M2[:, :], T.VAL[:, 15:143], col(E0 + 1), col(CW2), A.is_equal, A.mult))
+        else:
+            src, rd, c = {"W0": ("WA", "E", E0), "WP": ("WA", "CWP", CWP), "M1": ("ID", "NE", NE0 + 1), "MZ": ("ID", "NE", NE0)}[name]
+            copy(q, [src, rd], [name], T[name][:, :], T[src][:, :], col(c))
 
     def double(q, k):
         if k == 0:
-            copy(q, ["RW", "E"], ["PW"], T.PW[:, 0:128], T.RW[:, :], scale=col(E0 + 1))
+            op(q, ["RW", "E"], ["XT0_0"], lambda: V.tensor_scalar(T.XT[:, 0:128], T.RW[:, :], 16.0, col(E0 + 2), A.add, A.mult))
         else:
             n = 64 << k
-            copy(q, ["N0", "PW"], ["PW" if k < 4 else "PWb"], T.PW[:, n:2 * n], T.PW[:, 0:n], bias=T.N0[:, n >> 7:(n >> 7) + 1])
+            copy(q, ["N0", "XT0_0"], ["XT0_0" if k < 3 else "XT0_1"], T.XT[:, n:2 * n], T.XT[:, 0:n], bias=T.N0[:, n >> 7:(n >> 7) + 1])
 
-    def xt0(q, h):
-        copy(q, ["PW", "N0"], ["XT0_%d" % h], T.XT[:, 512 * h:512 * h + 512], T.PW[:, 512 * h:512 * h + 512], bias=T.N0[:, 16:17])
+    def zero(q):
+        op(q, [], ["PW"], lambda: V.memset(T.PW[:, :], 0.0))
 
-    def xt(q, t):
-        op(q, [], ["XT%d_0" % t, "XT%d_1" % t],
-           lambda: g.iota(T.XT[:, t * 1024:t * 1024 + 1024], [[1, 8], [0, 128]], 16 + 8 * t, 0, allow_small_or_imprecise_dtypes=True))
+    def unreacted(q):
+        dma(q, ["PW"], ["fld"], T.FD[0:128:16, :], T.PW[0:128:16, :])
 
-    def lo(q, t):
-        dma(q, ["XT0_0", "XT0_1"], ["XT%d_0" % t, "XT%d_1" % t], T.XT[1:128:16, t * 1024:t * 1024 + 1024], T.XT[1:128:16, 0:1024])
+    def xt(q, t, h):
+        a = t * 1024 + h * 512
+        op(q, [], ["XT%d_%d" % (t, h), "XZ%d_%d" % (t, h)],
+           lambda: g.iota(T.XT[:, a:a + 512], [[1, 4], [0, 128]], 8 * t + 4 * h, 0, allow_small_or_imprecise_dtypes=True))
+
+    def lo(q, t, h):
+        a = t * 1024 + h * 512
+        dma(q, ["XT0_0"], ["XT%d_%d" % (t, h)], T.XT[2:128:16, a:a + 512], T.XT[2:128:16, 0:512])
+        dma(q, ["XT0_0"], ["XZ%d_%d" % (t, h)], T.XT[0:128:16, a:a + 512], T.XT[0:128:16, 0:512])
 
     def narrow(q, h):
         copy(q, [("la32", "lb32")[h]], ["L%d" % h], (T.LA, T.LB)[h][:, :], (T.la32, T.lb32)[h][:, :])
 
     def scatter(q, t, a, b):
-        h = a // 2
-        op(q, ["XT%d_%d" % (t, h), "L%d" % h], ["PW", "PWb"],
-           lambda: V.tensor_copy(T.PW[:, :].indirect(lists(t, h, 16 * a - 32 * h, 16 * b - 32 * h)), T.XT[:, t * 1024 + 256 * a:t * 1024 + 256 * b]))
+        for h in range(2):
+            c, d = max(a, 2 * h), min(b, 2 * h + 2)
+            if c < d:
+                op(q, ["XT%d_%d" % (t, h), "XZ%d_%d" % (t, h), "L%d" % h], ["PW"],
+                   lambda: V.tensor_copy(T.PW[:, :].indirect(lists(t, h, 16 * c - 32 * h, 16 * d - 32 * h)), T.XT[:, t * 1024 + 256 * c:t * 1024 + 256 * d]))
 
     def pgather(q, t, h):
-        gather(q, ["PW", "L%d" % h], ["GP%d_%d" % (t, h)], T.GP[:, t * 1024 + h * 512:t * 1024 + h * 512 + 512], T.PW[:, :], lists(t, h))
+        gather(q, ["PW", "L%d" % h, "C64"], ["GP%d_%d" % (t, h)], T.GP[:, t * 1024 + h * 512:t * 1024 + h * 512 + 512], T.PW[:, :], lists(t, h),
+               None if h else col(C64))
+
+    def first(q, h):
+        gather(q, fill_res[:16] + ["T2_0", "L%d" % h], ["GP0_%d" % h], T.GP[:, h * 512:h * 512 + 512], T.T2[:, 0:P], lists(0, h), None if h else 64.0)
 
     def pwrap(q, t):
         if t < R:
@@ -304,44 +333,43 @@ def rank_program(g, core, T, topo):
         n = 64 if t < R else 128
         copy(q, [], ["PP", "PTR%d" % t], ptr(t, 0, n), T.PP[:, 0:n])
 
-    def first(q, h):
-        gather(q, ["fld", "L%d" % h], ["OLD0_%d" % h], T.OLD[:, 512 * h:512 * h + 512], T.ST[:, 0:P], lists(0, h))
-
     def sgather(q, t, a, b):
-        gather(q, sw_res(t) + ["PTR%d" % t], ["GS%d_%d" % (t, a)], T.GS[:, t * 1024 + 16 * a:t * 1024 + 16 * b], T.SW[:, 0:P + 1024 * t],
+        gather(q, sw_res(t) + ["PTR%d" % t], ["GS%d_%d" % (t, a)], T.GS[:, t * 1024 + 16 * a:t * 1024 + 16 * b], T.SW[:, 0:16 + 1024 * t],
                ptr(t, a, b), 64.0 if a < 32 else None)
+
+    def prewrap(q, t):
+        a = 0 if t < R - 1 else 32
+        wrap16(["GP%d_0" % t, "GP%d_1" % t], "PS%d" % (t % 2), 64 - a, "W0", "GP", t * 1024 + 16 * a, stop=False)
 
     def wrap(q, t):
         if t == 0:
-            wrap16(["OLD0_0", "OLD0_1"], "PS", 64, "W0", "OLD", 0)
+            wrap16(["GP0_0", "GP0_1"], "PS0", 64, "W0", "GP", 0)
         elif t < R - 1:
-            wrap16(["GS%d_0" % t, "GS%d_32" % t], "PS", 64, "W5", "GS", t * 1024)
+            wrap16(["GS%d_0" % t, "GS%d_32" % t], "PS%d" % (t % 2), 64, "WA", "GS", t * 1024, start=False)
         else:
-            wrap16(["GS3_32", "GS3_48"], "PS", 32, "W5", "GS", t * 1024 + 512)
+            wrap16(["GS3_32", "GS3_48"], "PS1", 32, "WA", "GS", t * 1024 + 512, start=False)
 
     def wrap_u(q):
-        wrap16(["GS3_0"], "PU", 32, "W5", "GS", 3 * 1024, False)
+        wrap16(["GP3_0"], "PU", 32, "W0", "GP", 3 * 1024, stop=False)
+        wrap16(["GS3_0"], "PU", 32, "WA", "GS", 3 * 1024, start=False, stop=False)
 
-    def post(q, t, h):
-        if h == 2:
-            copy(q, [], ["PS", "RXu%d" % t, "RXv%d" % t], T.RX[:, t * 4 + me, :], T.PS[:, 0:64])
-        elif t == 0:
-            copy(q, [], ["PS", "RX%s0" % "uv"[h]], T.RX[:, me, 32 * h:32 * h + 32], T.PS[:, 32 * h:32 * h + 32], scale=None if h else 64.0)
-        else:
-            copy(q, [], ["PS", "RXv3"], T.RX[:, 12 + me, 32:64], T.PS[:, 0:32])
+    def post(q, t):
+        a = 0 if t < R - 1 else 32
+        bank = "PS%d" % (t % 2)
+        copy(q, [], [bank, "RX%d" % t], T.RX[:, t * 4 + me, a:64], T[bank][:, 0:64 - a])
 
     def exchange(q, t):
         a = 0 if t < R - 1 else 32
-        cast(["RXu%d" % t, "RXv%d" % t][a // 32:], T.RX[:, t * 4 + me, a:64], T.RX[:, t * 4 + me, a:64], "ax%d" % t, "AX%d" % t, "sent0" if t == 0 else "sent")
+        cast(["RX%d" % t], T.RX[:, t * 4 + me, a:64], T.RX[:, t * 4 + me, a:64], "ax%d" % t, "AX%d" % t, "sent0" if t == 0 else "sent")
 
     def mine(q, t):
-        before(q, ["RXu%d" % t, "RXv%d" % t, "ID"], ["PU"])
+        before(q, ["RX%d" % t, "ID"], ["PU"])
         g.tensor.matmul(T.PU[:, 0:64], T.ID[:, :], T.RX[:, t * 4 + me, :], True, False)
 
     def join(q, t):
         halves = 2 if t < R - 1 else 1
-        rd = ["AX%d" % t, "RXv%d" % t, "ID"]
-        before(q, rd, ["open"])
+        rd = ["AX%d" % t, "RX%d" % t, "ID"]
+        before(q, rd, [])
         for h in range(halves):
             a = 32 * (1 - h) + 8 * me
             ins = g.tensor.matmul(T.PU[:, 32 * h:32 * h + 32], T.ID[:, :], T.RX[:, t * 4:t * 4 + 4, a:a + 8], False, h == halves - 1)
@@ -353,67 +381,92 @@ def rank_program(g, core, T, topo):
         copy(q, [], ["PU", "OFF%d" % t], T.OFF[:, t * 64:t * 64 + n], T.PU[:, 0:n])
 
     def new_u(q, t):
-        b = P + 1024 * t
-        gather(q, t2_res + ["OFF%d" % t, "E"], ["SW%d_4" % t], T.SW[:, b:b + 512], T.T2[:, :], T.OFF[:, t * 64:t * 64 + 32], col(E0 + 4))
+        b = 16 + 1024 * t
+        gather(q, t2_res + ["OFF%d" % t, "E"], ["SW%d_4" % t], T.SW[:, b:b + 512], T.T2[:, :], T.OFF[:, t * 64:t * 64 + 32], col(E0))
 
-    def new_v(q, t, c):
-        b = P + 1024 * t + 512 + 128 * c
-        gather(q, t2_res + ["OFF%d" % t, "E"], ["SW%d_%d" % (t, c)], T.SW[:, b:b + 128], T.T2[:, :],
-               T.OFF[:, t * 64 + 32 + 8 * c:t * 64 + 40 + 8 * c], col(E0 + c))
+    def new_v(q, t, a=0, b=N):
+        for c in range(a, b):
+            k = 16 + 1024 * t + 512 + 128 * c
+            gather(q, t2_res + ["OFF%d" % t, "E"], ["SW%d_%d" % (t, c)], T.SW[:, k:k + 128], T.T2[:, :],
+                   T.OFF[:, t * 64 + 32 + 8 * c:t * 64 + 40 + 8 * c], col(E0 + row[c]))
 
     def raw(q, t, k):
         a, b = (0, 4) if k == 4 else (turn[k], turn[k] + 1)
-        gather(q, ["LW", "OFF%d" % t], ["D%d_%d" % (t, turn.index(c)) for c in range(a, b)], T.D[:, t * 512 + 128 * a:t * 512 + 128 * b], T.LW[:, :],
-               T.OFF[:, t * 64 + 8 * a:t * 64 + 8 * b])
+        gather(q, lw_res + ["OFF%d" % t, "NE"], ["D%d_%d" % (t, turn.index(c)) for c in range(a, b)], dcol(t, a, b), T.LW[:, :],
+               T.OFF[:, t * 64 + 8 * a:t * 64 + 8 * b], None if t else col(NE0 + 1))
+
+    def mask_u(q, t):
+        b = 16 + 1024 * t
+        copy(q, ["D%d_%d" % (t, c) for c in range(N)] + ["E"], ["SW%d_4" % t], T.SW[:, b:b + 512], dcol(t, 0, N), col(E0))
 
     def ogather(q, t, h):
-        gather(q, st_res(t) + ["PTR%d" % t], ["OLD%d_%d" % (t, h)], T.OLD[:, t * 1024 + h * 512:t * 1024 + h * 512 + 512],
-               T.ST[:, 0:P + 1024 * t], ptr(t, 32 * h, 32 * h + 32))
+        gather(q, ew_res(t) + ["PTR%d" % t], ["OLD%d_%d" % (t, h)], T.OLD[:, t * 1024 + h * 512:t * 1024 + h * 512 + 512],
+               T.EW[:, 0:16 + 1024 * t], ptr(t, 32 * h, 32 * h + 32))
 
     def sum1(q, t):
         rd = ["D%d_%d" % (t, c) for c in range(N)] + ["OLD%d_0" % t, "M1", "MZ"]
         before(q, rd, ["PA"])
         g.tensor.matmul(T.PA[:, :], T.MZ[:, :], T.OLD[:, t * 1024:t * 1024 + 512], True, False)
-        g.tensor.matmul(T.PA[:, :], T.M1[:, :], T.D[:, t * 512:t * 512 + 512], False, True).then_inc(T.sem.cp, 1)
+        g.tensor.matmul(T.PA[:, :], T.M1[:, :], dcol(t, 0, N), False, True).then_inc(T.sem.cp, 1)
         after(q, "cp", 1, rd, ["PA"])
 
-    banks = ["PB", "PC", "PD", "PE"]
+    banks = ["PB", "PC"]
 
     def open2(q, t):
-        before(q, ["OLD%d_1" % t, "MZ"], banks)
-        for k in range(N):
-            a = t * 1024 + 512 + 128 * turn[k]
-            g.tensor.matmul(T[banks[k]][:, 0:128], T.MZ[:, :], T.OLD[:, a:a + 128], True, False)
+        before(q, ["OLD%d_1" % t, "MZ"] if t else sw_res(1) + ["WA"], banks)
+        for k in range(2):
+            a = t * 1024 + 512 + 256 * k
+            if t:
+                g.tensor.matmul(T[banks[k]][:, 0:256], T.MZ[:, :], T.OLD[:, a:a + 256], True, False)
+            else:
+                g.tensor.matmul(T[banks[k]][:, 0:256], T.WA[:, 15:143], T.SW[:, 16 + a:16 + a + 256], True, False)
 
-    def close2(q, t, k):
-        c = turn[k]
-        rd = ["D%d_3" % t if c == me else "DL%d" % t, "M2"]
-        before(q, rd, ["open%d" % k])
-        d = T.D[:, t * 512 + 128 * c:t * 512 + 128 * c + 128] if c == me else T.DL[:, t * 4 + c]
-        g.tensor.matmul(T[banks[k]][:, 0:128], T.M2[:, :], d, False, True).then_inc(T.sem.cp, 1)
-        after(q, "cp", 1, rd, [banks[k]])
+    def close2(q, t):
+        order = [me, me ^ 1] + [c for c in range(N) if c // 2 != me // 2]
+        for i, c in enumerate(order):
+            before(q, ["D%d_3" % t if c == me else "DL%d" % t, "M2"], [])
+            ins = g.tensor.matmul(T[banks[c // 2]][:, 128 * (c % 2):128 * (c % 2) + 128], T.M2[:, :],
+                                  dcol(t, c, c + 1) if c == me else T.DL[:, t * 4 + c], False, i % 2 == 1)
+            if i % 2:
+                ins.then_inc(T.sem.cp, 1)
+                after(q, "cp", 1, ["D%d_3" % t, "DL%d" % t, "M2"], [banks[c // 2]])
 
     def keep1(q, t):
-        copy(q, [], ["PA", "ST%d_0" % t], T.ST[:, P + 1024 * t:P + 1024 * t + 512], T.PA[:, :])
+        copy(q, [], ["PA", "EW%d_0" % t], T.EW[:, 16 + 1024 * t:16 + 1024 * t + 512], T.PA[:, :])
 
     def keep2(q, t, k):
-        b = P + 1024 * t + 512 + 128 * turn[k]
-        copy(q, [], [banks[k], "ST%d_%d" % (t, k + 1)], T.ST[:, b:b + 128], T[banks[k]][:, 0:128])
+        b = 16 + 1024 * t + 512 + 256 * k
+        copy(q, [], [banks[k], "EW%d_%d" % (t, k + 1)], T.EW[:, b:b + 256], T[banks[k]][:, 0:256])
 
     def final(q, k):
         a, b = CUTS[k], CUTS[k + 1]
-        gather(q, st_res(R) + ["PTR4"], ["OUT%d" % k], T.OUT[:, 16 * a:16 * b], T.ST[:, :], ptr(R, a, b))
+        op(q, ew_res(R) + ["PTR4", "fld"], ["OUT%d" % k],
+           lambda: V.tensor_tensor(T.OUT[:, 16 * a:16 * b], T.EW[:, :].indirect(ptr(R, a, b)), T.FD[:, 16 * a:16 * b], A.add))
 
-    def store(q, k):
-        a, b = 16 * CUTS[2 * k], 16 * CUTS[2 * k + 2]
-        dma(q, ["OUT%d" % (2 * k), "OUT%d" % (2 * k + 1)], ["y%d" % k], T.y[:, a:b], T.OUT[:, a:b])
+    def last(q, k, stage):
+        a, b = CUTS[k], CUTS[k + 1]
+        bank, n = ("PD", "PS0")[k % 2], 16 * (b - a)
+        got = T.OLD[:, 512 * (k % 2):512 * (k % 2) + n]
+        if stage == 0:
+            gather(q, ew_res(R) + ["PTR4"], ["G%d" % k], got, T.EW[:, :], ptr(R, a, b))
+        elif stage == 1:
+            before(q, ["fld", "ID"], [bank])
+            g.tensor.matmul(T[bank][:, 0:n], T.ID[:, :], T.FD[:, 16 * a:16 * b], True, False)
+            before(q, ["G%d" % k], [])
+            g.tensor.matmul(T[bank][:, 0:n], T.ID[:, :], got, False, True).then_inc(T.sem.cp, 1)
+            after(q, "cp", 1, ["fld", "ID", "G%d" % k], [bank])
+        else:
+            copy(q, [], [bank, "OUT%d" % k], T.OUT[:, 16 * a:16 * b], T[bank][:, 0:n])
 
-    steps = {"load": load, "iota": iota, "rows_out": rows_out, "rows_in": rows_in, "start_sw": start_sw, "fill": fill, "const": const,
-             "mat": mat, "double": double, "xt0": xt0, "xt": xt, "lo": lo, "narrow": narrow, "scatter": scatter, "pgather": pgather,
-             "pwrap": pwrap, "pcast": pcast, "first": first, "sgather": sgather, "wrap": wrap, "wrap_u": wrap_u, "post": post,
-             "exchange": exchange, "mine": mine, "join": join, "offsets": offsets, "new_u": new_u, "new_v": new_v, "raw": raw,
-             "send": send, "ogather": ogather, "sum1": sum1, "open2": open2, "close2": close2, "keep1": keep1, "keep2": keep2,
-             "final": final, "store": store}
+    def store(q, a, b):
+        dma(q, ["OUT%d" % k for k in range(a, b)], ["y%d" % a], T.y[:, 16 * CUTS[a]:16 * CUTS[b]], T.OUT[:, 16 * CUTS[a]:16 * CUTS[b]])
+
+    steps = {"load": load, "own": own, "law": law, "species": species, "iota": iota, "rows_out": rows_out, "rows_in": rows_in, "fill": fill,
+             "const": const, "mat": mat, "double": double, "zero": zero, "unreacted": unreacted, "xt": xt, "lo": lo, "narrow": narrow,
+             "scatter": scatter, "pgather": pgather, "first": first, "pwrap": pwrap, "pcast": pcast, "sgather": sgather, "prewrap": prewrap, "wrap": wrap,
+             "wrap_u": wrap_u, "post": post, "exchange": exchange, "mine": mine, "join": join, "offsets": offsets, "new_u": new_u,
+             "new_v": new_v, "raw": raw, "mask_u": mask_u, "send": send, "ogather": ogather, "sum1": sum1, "open2": open2,
+             "close2": close2, "keep1": keep1, "keep2": keep2, "final": final, "last": last, "store": store}
     for task in ORDER:
         steps[task[0]](*task[1:])
     for sem in sorted(total):

@@ -1,14 +1,14 @@
 from concourse.bass import DstId, RemoteDMATransfer
 from concourse.mybir import AluOpType as A, ActivationFunctionType as F
 
-N, P, R = 4, 2048, 4
+N, P, R, Z = 4, 2048, 4, 128
 BF, F32, I32, U16 = "bfloat16", "float32", "int32", "uint16"
 SCRATCH = {
-    "la32": ("sbuf", [128, 128], I32), "lb32": ("sbuf", [128, 128], I32),
-    "LA": ("sbuf", [128, 128], U16), "LB": ("sbuf", [128, 128], U16),
+    "la32": ("sbuf", [128, 4, 32], I32), "lb32": ("sbuf", [128, 4, 32], I32),
+    "L": ("sbuf", [128, 4, 64], U16),
     "FD": ("sbuf", [128, 2048], BF),
-    "EW": ("sbuf", [128, 4112], BF),
-    "SW": ("sbuf", [128, 3088], BF),
+    "EW": ("sbuf", [128, 4224], BF),
+    "SW": ("sbuf", [128, 3200], BF),
     "T2": ("sbuf", [128, 4096], BF),
     "LW": ("sbuf", [128, 4096], BF),
     "PW": ("sbuf", [128, 2048], BF),
@@ -19,41 +19,42 @@ SCRATCH = {
     "RX": ("sbuf", [128, 16, 64], BF),
     "OFF": ("sbuf", [128, 256], U16), "PTR": ("sbuf", [128, 384], U16),
     "OUT": ("sbuf", [128, 2048], F32),
-    "RW": ("sbuf", [128, 128], F32), "PK": ("sbuf", [128, 4], I32), "KM": ("sbuf", [128, 4], I32),
-    "VAL": ("sbuf", [128, 144], F32), "COL": ("sbuf", [128, 16], F32), "N0": ("sbuf", [128, 8], F32),
+    "RW": ("sbuf", [128, 144], F32), "PK": ("sbuf", [128, 4], I32), "KM": ("sbuf", [128, 4], I32),
+    "K15": ("sbuf", [128, 4], F32), "COL": ("sbuf", [128, 16], F32), "N0": ("sbuf", [128, 8], F32),
     "W0": ("sbuf", [128, 144], BF), "WA": ("sbuf", [128, 144], BF), "WP": ("sbuf", [128, 144], BF),
     "M1": ("sbuf", [128, 128], BF), "MZ": ("sbuf", [128, 128], BF), "M2": ("sbuf", [128, 128], BF), "ID": ("sbuf", [128, 128], BF),
     "R1": ("dram", [128, 256], BF), "RL": ("dram", [4, 128, 256], BF),
     "PS0": ("psum", [128, 512], F32), "PS1": ("psum", [128, 512], F32), "PU": ("psum", [128, 512], F32), "PP": ("psum", [128, 512], F32),
     "PA": ("psum", [128, 512], F32), "PB": ("psum", [128, 512], F32), "PC": ("psum", [128, 512], F32), "PD": ("psum", [128, 512], F32),
 }
-SEMAPHORES = (["cv", "cs", "cp", "cg", "sent0", "sent", "at2"] + ["ax%d" % t for t in range(R)] + ["ad%d" % t for t in range(R)]
+SEMAPHORES = (["cv", "cs", "cp", "cg", "sent0", "sent"] + ["at%d" % r for r in range(N)] + ["ax%d" % t for t in range(R)] + ["ad%d" % t for t in range(R)]
               + ["m%d" % k for k in range(36)])
 
 PLAN = """
-load y r1; load y la; load y lb; iota g PK; iota g RW; iota g VAL; fill v 0 4; fill s 4 8; fill s 8 16; fill y 16 24; zero v; species y PW;
-const v KF; const v E; double v 0; const s N0; double s 1; double s 2; mat v WA; mat v ID; const s CWP; mat s W0; const s NE; mat s WP; const s C64;
-narrow v 0; narrow v 1; const v EW; species y T2; first s 1; first s 0; wrap p 0; post s 0; mine p 0; fill y 24 32; own y 16; double v 3;
-scatter v 0 0 4; pgather v 1 1; const v SW; rows_out g; xt g 1 0; exchange g 0; xt g 1 1; rows_in y; lo y 1 0; lo y 1 1; join p 0;
-offsets v 0; new_u v 0; const s CW2; mat s MZ; mat s M1; pgather s 1 0; pwrap p 1; pcast v 1; new_v s 0;
+load y r1; load y la; load y lb; iota g PK; iota g RW; iota g K15; fill v 0 8; fill s 8 16; species y T2; const v KM; zero v 2 3;
+const v KF; zero v 3 4; const v E; zero v 0 2; species y PW; fill y 16 32; const s N0; double s 0; double s 2; double s 4; double s 6;
+narrow v 0; narrow v 1; first s 0; first s 1; double v 1; double v 3; mat v WA; double v 5; double v 7; scatter v 0 0 4; mat v ID; own y 16;
+pgather v 1 2 4; rows_out g; xt g 1 0; rows_in y; wrap p 0; const s CWP; const s SW; const s EW; mat s WP; post s 0; mine p 0; exchange g 0; join p 0; offsets v 0;
+xt g 1 1; lo y 1 0; lo y 1 1; xt g 2 0; xt g 2 1; pgather s 1 0 2; const s NE; new_u v 0; new_v s 0; pwrap p 1; pcast v 1;
 
-law y 0 2 sent0; law y 2 4; xt g 2 0; xt g 2 1; lo y 2 0; lo y 2 1; sgather s 1 0 32; sgather s 1 32 64; prewrap p 1; wrap p 1; post s 1; exchange g 1;
-scatter v 1 0 2; mat v M2; scatter v 1 2 4; open2 p 0; mine p 1; raw s 0 4; send g 0 0; send g 0 1; xt g 3 0; xt g 3 1; lo y 3 0; lo y 3 1;
-pgather v 2 1; pgather s 2 0; join p 1; offsets v 1; pwrap p 2; raw v 1 4; new_v s 1; mask_u v 1; pcast v 2; send g 1 0; send g 1 1;
+sgather s 1 48 64; sgather s 1 0 32; scatter v 1 0 1; sgather v 1 32 48; wrap p 1; const s CW2; mat s M2; post s 1; law y 0 2 sent0; law y 2 4; raw s 0 0 4; lo y 2 0;
+lo y 2 1; exchange g 1; mat y M2row; send g 0 0; send g 0 1; xt g 3 0; lo y 3 0; scatter v 1 1 4; pgather s 2 0 2; pgather v 2 2 4; mine p 1; join p 1;
+offsets v 1; new_v s 1; raw v 1 0 4; send g 1 0; send g 1 1; xt g 3 1; lo y 3 1; pwrap p 2; pcast v 2; mat s M1; mask_u v 1;
 
-sgather s 2 0 32; sgather s 2 32 64; prewrap p 2; close2 p 0; wrap p 2; keep2 s 0 0; keep2 s 0 1; post s 2; exchange g 2; mine p 2;
-scatter v 2 0 4; ogather s 1 1; ogather s 1 0; open2 p 1; close2 p 1; load y fld AX2;
-pgather v 3 0; pgather s 3 1; join p 2; offsets v 2; pwrap p 3; raw v 2 4; new_v s 2; pcast v 3; mask_u v 2; send g 2 0; send g 2 1; keep2 s 1 0;
+sgather s 2 48 64; sgather s 2 0 32; scatter v 2 0 1; sgather v 2 32 48; open2 p 0; close2 p 0; keep2 s 0 0; keep2 s 0 1; wrap p 2; post s 2; mine p 2; ogather s 1 0;
+ogather s 1 1; open2 p 1; scatter v 2 1 4; pgather v 3 2 4; pgather s 3 0 2; exchange g 2; load y fld AX2; unreacted y; join p 2; offsets v 2;
+raw v 2 0 4; send g 2 0; new_v s 2; close2 p 1; keep2 s 1 0; pwrap p 3; pcast v 3; sum1 p 1; mask_u v 2;
 
-sgather v 3 48 64; sgather s 3 32 48; sum1 p 1; prewrap p 3; wrap p 3; sgather s 3 0 32; keep2 s 1 1; post s 3; exchange g 3; wrap_u p;
-scatter v 3 0 4; unreacted y; keep1 s 1; ogather s 2 0; ogather s 2 1; sum1 p 2; keep1 s 2; join p 3; offsets v 3;
+sgather s 3 32 48; keep2 v 1 1; sgather v 3 48 64; wrap p 3; keep1 v 1; sgather s 3 0 32; post s 3; exchange g 3; scatter v 3 0 3;
+ogather s 2 0; ogather s 2 1; sum1 p 2; keep1 s 2; send g 2 1; wrap_u p; join p 3; offsets v 3;
 
-raw v 3 0; raw s 3 1; send g 3 0; open2 p 2; close2 p 2; keep2 s 2 1; keep2 v 2 0; raw v 3 2; send g 3 1; pwrap p 4; raw s 3 3;
-ogather v 3 0; ogather s 3 1; sum1 p 3; open2 p 3; keep1 s 3; pcast v 4; close2 p 3; keep2 v 3 0; keep2 s 3 1;
-final v 0; last s 3 0; store y 0 1; last p 3 1; final v 1; store y 1 2; last s 4 0; last p 4 1; last s 3 2; final v 2; store y 2 4; last s 4 2; store y 4 5
+raw s 3 0; raw v 3 1; send g 3 0; open2 p 2; close2 p 2; scatter v 3 3 4; pwrap p 4; keep2 s 2 1; keep2 s 2 0; raw v 3 2; send g 3 1; raw s 3 3;
+ogather s 3 0; ogather v 3 1; pcast v 4; sum1 p 3; keep1 v 3; open2 p 3; close2 p 3; pwrap p 5; keep2 s 3 1; keep2 v 3 0;
+last s 2 0; final v 0; pcast v 5; store y 0 1; final v 1; store y 1 2; last s 5 0; last p 2 1; last p 5 1; last s 2 2; final v 3;
+store y 2 4; last s 5 2; final v 4; store y 4 6
 """
 ORDER = [tuple(int(w) if w.isdigit() else w for w in x.split()) for x in PLAN.split(";")]
-CUTS = [0, 16, 40, 72, 96, 128]
+CUTS = [0, 8, 36, 64, 88, 112, 128]
 
 
 def rank_program(g, core, T, topo):
@@ -129,7 +130,7 @@ def rank_program(g, core, T, topo):
     turn = [r for part in deal(me) for r, es in part] + [me]
 
     def dcol(t, a, b):
-        return T.D[:, t * 512 + 128 * a:t * 512 + 128 * b] if t else T.EW[:, 16 + 128 * a:16 + 128 * b]
+        return T.D[:, t * 512 + 128 * a:t * 512 + 128 * b] if t else T.EW[:, Z + 128 * a:Z + 128 * b]
 
     def send(q, t, k):
         part = deal(me)[k]
@@ -143,7 +144,7 @@ def rank_program(g, core, T, topo):
             writer["DL%d" % t] = ("ad%d" % t, total["ad%d" % t], {})
 
     V, S = g.vector, g.scalar
-    KF, E0, NE0, C64, CWP, CW2 = 0, 1, 6, 8, 9, 10
+    KF, E0, NE0, CWP, CW2 = 0, 1, 6, 8, 9
 
     def col(k):
         return T.COL[:, k:k + 1]
@@ -184,8 +185,8 @@ def rank_program(g, core, T, topo):
             ins.then_inc(T.sem.cp, 1)
             after("p", "cp", 1, rd + [w], [bank])
 
-    def lists(t, h, a=0, b=32):
-        return (T.LA, T.LB)[h][:, 32 * t + a:32 * t + b]
+    def members(t, a, b):
+        return T.L[:, t, 16 * a:16 * b], sorted({a // 2, (b - 1) // 2})
 
     def ptr(t, a, b):
         return T.PTR[:, 64 * (t - 1) + a:64 * (t - 1) + b]
@@ -206,14 +207,14 @@ def rank_program(g, core, T, topo):
         if what == "r1":
             dma(q, [], ["R1"], T.R1[:, :], T.law[1:128:16, :])
         elif what == "la":
-            dma(q, [], ["la32"], T.la32[:, :], T.la[:, :])
+            dma(q, [], ["la32"], T.la32[:], T.la[:, :])
         elif what == "lb":
-            dma(q, [], ["lb32"], T.lb32[:, :], T.lb[:, :])
+            dma(q, [], ["lb32"], T.lb32[:], T.lb[:, :])
         else:
             dma(q, [], ["fld"], T.FD[:, :], T.fld[:, :])
 
-    def own(q, a):
-        for r in range(2):
+    def own(q, a, r0=0):
+        for r in range(r0, 2):
             dma(q, fill_res[:a], ["T2_%d" % r], T.T2[r:128:16, 0:128 * a], T.law[r:128:16, 0:128 * a])
 
     def law(q, a, b, gate=None):
@@ -222,7 +223,7 @@ def rank_program(g, core, T, topo):
 
     def species(q, where):
         if where == "PW":
-            dma(q, [], ["PW"], T.PW[0:128:16, :], T.fld[0:128:16, :])
+            dma(q, ["PW%d" % k for k in range(4)], ["PW"], T.PW[0:128:16, :], T.fld[0:128:16, :])
         else:
             dma(q, fill_res[:16], ["T2_0"], T.T2[0:128:16, 0:P], T.fld[0:128:16, :])
 
@@ -230,16 +231,20 @@ def rank_program(g, core, T, topo):
         if what == "PK":
             op(q, [], ["PK"], lambda: g.iota(T.PK[:, 0:1], [[0, 1]], 0, 1))
         elif what == "RW":
-            op(q, [], ["RW"], lambda: g.iota(T.RW[:, :], [[1, 128]], 0, 0, allow_small_or_imprecise_dtypes=True))
+            op(q, [], ["RW"], lambda: g.iota(T.RW[:, :], [[1, 144]], 0, 0, allow_small_or_imprecise_dtypes=True))
         else:
-            op(q, [], ["VAL"], lambda: g.iota(T.VAL[:, :], [[-1, 144]], 15, 1, allow_small_or_imprecise_dtypes=True))
+            op(q, [], ["K15"], lambda: g.iota(T.K15[:, 0:1], [[0, 1]], 15, 1, allow_small_or_imprecise_dtypes=True))
 
     def rows_out(q):
-        cast(["R1"], T.R1[:, :], T.RL[me], "at2", "RL", "sent")
+        cast(["R1"], T.R1[:, :], T.RL[me], "at%d" % me, "RL", "sent")
+        del total["at%d" % me]
+        for r in others:
+            total["at%d" % r] = ne
+            writer["RL%d" % r] = ("at%d" % r, ne, {})
 
     def rows_in(q):
-        for r in others:
-            dma(q, ["RL"] + fill_res, ["T2_%d" % row[r]], T.T2[row[r]:128:16, :], T.RL[r])
+        for r in others[::-1]:
+            dma(q, ["RL%d" % r] + fill_res, ["T2_%d" % row[r]], T.T2[row[r]:128:16, :], T.RL[r])
 
     def fill(q, a, b):
         out = T.T2[:, 128 * a:128 * b]
@@ -253,105 +258,94 @@ def rank_program(g, core, T, topo):
             copy(q, fill_res[:b - a], fill_res[a:b], out, T.T2[:, 0:128 * (b - a)])
 
     def const(q, k):
-        if k == "KF":
+        if k == "KM":
             op(q, ["PK"], ["KM"], lambda: V.tensor_scalar(T.KM[:, 0:1], T.PK[:, 0:1], 15, None, A.bitwise_and))
+        elif k == "KF":
             copy(q, ["KM"], ["KF"], col(KF), T.KM[:, 0:1])
         elif k == "E":
             op(q, ["RW", "KF"], ["E"], lambda: V.tensor_scalar(T.COL[:, E0:E0 + 5], T.RW[:, 0:5], col(KF), None, A.is_equal))
         elif k == "N0":
-            copy(q, ["RW", "E"], [k], T.N0[:, :], T.RW[:, 0:8], col(E0 + 1))
-        elif k == "C64":
-            copy(q, ["E"], [k], col(C64), col(E0), 63.0, 1.0)
+            copy(q, ["RW", "E"], [k], T.N0[:, :], T.RW[:, 1:9], col(E0 + 1))
         elif k == "CWP":
-            copy(q, ["E"], [k], col(CWP), col(E0 + 1), 128.0, col(E0 + 2))
+            copy(q, ["E"], [k], col(CWP), col(E0 + 1), 128.0, col(E0))
         elif k == "NE":
             copy(q, ["E"], [k], T.COL[:, NE0:NE0 + 2], T.COL[:, E0:E0 + 2], -1.0, 1.0)
         elif k == "CW2":
-            copy(q, ["E", "NE"], [k], col(CW2), col(NE0), -0.5, col(E0 + 1))
+            copy(q, ["E", "NE"], [k], col(CW2), col(NE0 + 1), -1.0, col(E0))
         else:
-            op(q, [], [k], lambda: V.memset(T[k][:, 0:16], 0.0))
+            copy(q, ["RW", "E"], [k], T[k][:, 0:Z], T.RW[:, 0:Z], col(E0))
 
     def mat(q, name):
         if name == "WA":
-            op(q, ["VAL", "KF"], [name], lambda: V.tensor_scalar(T.WA[:, :], T.VAL[:, :], col(KF), None, A.is_equal))
+            op(q, ["RW", "KF", "K15"], [name], lambda: V.tensor_scalar(T.WA[:, :], T.RW[:, :], col(KF), T.K15[:, 0:1], A.add, A.is_equal))
         elif name == "ID":
-            op(q, ["VAL"], [name], lambda: V.tensor_scalar(T.ID[:, :], T.VAL[:, 15:143], 0.0, None, A.is_equal))
-        elif name == "M2":
-            copy(q, ["CW2"], ["CW2"], col(CW2), col(CW2), 2.0)
-            op(q, ["VAL", "E", "CW2"], [name], lambda: V.tensor_scalar(T.M2[:, :], T.VAL[:, 15:143], col(E0 + 1), col(CW2), A.is_equal, A.mult))
+            op(q, ["RW", "K15"], [name], lambda: V.tensor_scalar(T.ID[:, :], T.RW[:, 15:143], T.K15[:, 0:1], None, A.is_equal))
+        elif name == "M2row":
+            dma(q, ["WA"], ["M2"], T.M2[1:128:16, :], T.WA[1:128:16, 15:143])
         else:
-            src, rd, c = {"W0": ("WA", "E", E0), "WP": ("WA", "CWP", CWP), "M1": ("ID", "NE", NE0 + 1), "MZ": ("ID", "NE", NE0)}[name]
+            src, rd, c = {"WP": ("WA", "CWP", CWP), "M1": ("ID", "NE", NE0 + 1), "M2": ("ID", "CW2", CW2)}[name]
             copy(q, [src, rd], [name], T[name][:, :], T[src][:, :], col(c))
 
     def double(q, k):
-        if k == 0:
-            op(q, ["RW", "E"], ["XT0_0"], lambda: V.tensor_scalar(T.XT[:, 0:128], T.RW[:, :], 16.0, col(E0 + 2), A.add, A.mult))
-        else:
-            n = 64 << k
-            copy(q, ["N0", "XT0_0"], ["XT0_0" if k < 3 else "XT0_1"], T.XT[:, n:2 * n], T.XT[:, 0:n], bias=T.N0[:, n >> 7:(n >> 7) + 1])
+        copy(q, ["RW", "E", "N0"], ["XT0_%d" % k], T.XT[:, 128 * k:128 * k + 128], T.RW[:, 0:128], col(E0), T.N0[:, k:k + 1])
 
-    def zero(q):
-        op(q, [], ["PW"], lambda: V.memset(T.PW[:, :], 0.0))
+    def zero(q, a, b):
+        op(q, [], ["PW%d" % k for k in range(a, b)], lambda: V.memset(T.PW[:, 512 * a:512 * b], 0.0))
 
     def unreacted(q):
-        dma(q, ["PW"], ["fld"], T.FD[0:128:16, :], T.PW[0:128:16, :])
+        dma(q, fill_res[:16], ["fld"], T.FD[0:128:16, :], T.T2[5:128:16, 0:P])
 
     def xt(q, t, h):
         a = t * 1024 + h * 512
-        op(q, [], ["XT%d_%d" % (t, h), "XZ%d_%d" % (t, h)],
-           lambda: g.iota(T.XT[:, a:a + 512], [[1, 4], [0, 128]], 8 * t + 4 * h, 0, allow_small_or_imprecise_dtypes=True))
+        op(q, [], ["XT%d_%d" % (t, h)],
+           lambda: g.iota(T.XT[:, a:a + 512], [[1, 4], [0, 128]], 1 + 8 * t + 4 * h, 0, allow_small_or_imprecise_dtypes=True))
 
     def lo(q, t, h):
         a = t * 1024 + h * 512
-        dma(q, ["XT0_0"], ["XT%d_%d" % (t, h)], T.XT[2:128:16, a:a + 512], T.XT[2:128:16, 0:512])
-        dma(q, ["XT0_0"], ["XZ%d_%d" % (t, h)], T.XT[0:128:16, a:a + 512], T.XT[0:128:16, 0:512])
+        dma(q, ["XT0_%d" % k for k in range(4)], ["XT%d_%d" % (t, h)], T.XT[0:128:16, a:a + 512], T.XT[0:128:16, 0:512])
 
     def narrow(q, h):
-        copy(q, [("la32", "lb32")[h]], ["L%d" % h], (T.LA, T.LB)[h][:, :], (T.la32, T.lb32)[h][:, :])
+        copy(q, [("la32", "lb32")[h]], ["L%d" % h], T.L[:, :, 32 * h:32 * h + 32], (T.la32, T.lb32)[h][:])
 
     def scatter(q, t, a, b):
-        for h in range(2):
-            c, d = max(a, 2 * h), min(b, 2 * h + 2)
-            if c < d:
-                op(q, ["XT%d_%d" % (t, h), "XZ%d_%d" % (t, h), "L%d" % h], ["PW"],
-                   lambda: V.tensor_copy(T.PW[:, :].indirect(lists(t, h, 16 * c - 32 * h, 16 * d - 32 * h)), T.XT[:, t * 1024 + 256 * c:t * 1024 + 256 * d]))
+        off, hs = members(t, a, b)
+        op(q, ["XT%d_%d" % (t, h) for h in (hs if t else range(2 * a, 2 * b))] + ["L%d" % h for h in hs], ["PW"],
+           lambda: V.tensor_copy(T.PW[:, :].indirect(off), T.XT[:, t * 1024 + 256 * a:t * 1024 + 256 * b]))
 
-    def pgather(q, t, h):
-        gather(q, ["PW", "L%d" % h, "C64"], ["GP%d_%d" % (t, h)], T.GP[:, t * 1024 + h * 512:t * 1024 + h * 512 + 512], T.PW[:, :], lists(t, h),
-               None if h else col(C64))
+    def gp_res(t, a=0, b=4):
+        return ["GP%d_%d" % (t, k) for k in range(a, b)]
+
+    def pgather(q, t, a, b):
+        off, hs = members(t, a, b)
+        gather(q, ["PW"] + ["L%d" % h for h in hs], gp_res(t, a, b), T.GP[:, t * 1024 + 256 * a:t * 1024 + 256 * b], T.PW[:, :], off)
 
     def first(q, h):
-        gather(q, fill_res[:16] + ["T2_0", "L%d" % h], ["GP0_%d" % h], T.GP[:, h * 512:h * 512 + 512], T.T2[:, 0:P], lists(0, h), None if h else 64.0)
+        gather(q, fill_res[:16] + ["T2_0", "L%d" % h], gp_res(0, 2 * h, 2 * h + 2), T.GP[:, h * 512:h * 512 + 512], T.T2[:, 0:P], members(0, 2 * h, 2 * h + 2)[0], None if h else 64.0)
 
     def pwrap(q, t):
         if t < R:
-            wrap16(["GP%d_0" % t, "GP%d_1" % t], "PP", 64, "WP", "GP", t * 1024)
+            wrap16(gp_res(t), "PP", 64, "WP", "GP", t * 1024)
         else:
-            wrap16(["PW"], "PP", 128, "WP", "PW", 0)
+            wrap16(["PW"], "PP" if t == R else "PS1", 64, "WP", "PW", 1024 * (t - R))
 
     def pcast(q, t):
-        n = 64 if t < R else 128
-        copy(q, [], ["PP", "PTR%d" % t], ptr(t, 0, n), T.PP[:, 0:n])
+        bank = "PP" if t <= R else "PS1"
+        copy(q, [], [bank, "PTR%d" % t], ptr(t, 0, 64), T[bank][:, 0:64])
 
     def sgather(q, t, a, b):
-        gather(q, sw_res(t) + ["PTR%d" % t], ["GS%d_%d" % (t, a)], T.GS[:, t * 1024 + 16 * a:t * 1024 + 16 * b], T.SW[:, 0:16 + 1024 * t],
+        gather(q, sw_res(t) + ["PTR%d" % t], ["GS%d_%d" % (t, k) for k in range(a, b, 16)], T.GS[:, t * 1024 + 16 * a:t * 1024 + 16 * b], T.SW[:, 0:Z + 1024 * t],
                ptr(t, a, b), 64.0 if a < 32 else None)
-
-    def prewrap(q, t):
-        a = 0 if t < R - 1 else 32
-        wrap16(["GP%d_0" % t, "GP%d_1" % t], "PS%d" % (t % 2), 64 - a, "W0", "GP", t * 1024 + 16 * a, stop=False)
 
     def wrap(q, t):
         if t == 0:
-            wrap16(["GP0_0", "GP0_1"], "PS0", 64, "W0", "GP", 0)
+            wrap16(gp_res(0), "PS0", 64, "WA", "GP", 0)
         elif t < R - 1:
-            wrap16(["GS%d_0" % t, "GS%d_32" % t], "PS%d" % (t % 2), 64, "WA", "GS", t * 1024, start=False)
+            wrap16(["GS%d_%d" % (t, k) for k in range(0, 64, 16)], "PS%d" % (t % 2), 64, "WA", "GS", t * 1024)
         else:
-            wrap16(["GS3_32", "GS3_48"], "PS1", 32, "WA", "GS", t * 1024 + 512, start=False)
+            wrap16(["GS3_32", "GS3_48"], "PS1", 32, "WA", "GS", t * 1024 + 512)
 
     def wrap_u(q):
-        wrap16(["GP3_0"], "PU", 32, "W0", "GP", 3 * 1024, stop=False)
-        wrap16(["GS3_0"], "PU", 32, "WA", "GS", 3 * 1024, start=False, stop=False)
+        wrap16(["GS3_0", "GS3_16"], "PU", 32, "WA", "GS", 3 * 1024, stop=False)
 
     def post(q, t):
         a = 0 if t < R - 1 else 32
@@ -381,45 +375,45 @@ def rank_program(g, core, T, topo):
         copy(q, [], ["PU", "OFF%d" % t], T.OFF[:, t * 64:t * 64 + n], T.PU[:, 0:n])
 
     def new_u(q, t):
-        b = 16 + 1024 * t
+        b = Z + 1024 * t
         gather(q, t2_res + ["OFF%d" % t, "E"], ["SW%d_4" % t], T.SW[:, b:b + 512], T.T2[:, :], T.OFF[:, t * 64:t * 64 + 32], col(E0))
 
     def new_v(q, t, a=0, b=N):
         for c in range(a, b):
-            k = 16 + 1024 * t + 512 + 128 * c
+            k = Z + 1024 * t + 512 + 128 * c
             gather(q, t2_res + ["OFF%d" % t, "E"], ["SW%d_%d" % (t, c)], T.SW[:, k:k + 128], T.T2[:, :],
                    T.OFF[:, t * 64 + 32 + 8 * c:t * 64 + 40 + 8 * c], col(E0 + row[c]))
 
-    def raw(q, t, k):
-        a, b = (0, 4) if k == 4 else (turn[k], turn[k] + 1)
+    def raw(q, t, a, b=None):
+        a, b = (a, b) if b else (turn[a], turn[a] + 1)
         gather(q, lw_res + ["OFF%d" % t, "NE"], ["D%d_%d" % (t, turn.index(c)) for c in range(a, b)], dcol(t, a, b), T.LW[:, :],
                T.OFF[:, t * 64 + 8 * a:t * 64 + 8 * b], None if t else col(NE0 + 1))
 
     def mask_u(q, t):
-        b = 16 + 1024 * t
+        b = Z + 1024 * t
         copy(q, ["D%d_%d" % (t, c) for c in range(N)] + ["E"], ["SW%d_4" % t], T.SW[:, b:b + 512], dcol(t, 0, N), col(E0))
 
     def ogather(q, t, h):
-        gather(q, ew_res(t) + ["PTR%d" % t], ["OLD%d_%d" % (t, h)], T.OLD[:, t * 1024 + h * 512:t * 1024 + h * 512 + 512],
-               T.EW[:, 0:16 + 1024 * t], ptr(t, 32 * h, 32 * h + 32))
+        gather(q, ew_res(t) + ["PTR%d" % t, "NE"], ["OLD%d_%d" % (t, h)], T.OLD[:, t * 1024 + h * 512:t * 1024 + h * 512 + 512],
+               T.EW[:, 0:Z + 1024 * t], ptr(t, 32 * h, 32 * h + 32), col(NE0))
 
     def sum1(q, t):
-        rd = ["D%d_%d" % (t, c) for c in range(N)] + ["OLD%d_0" % t, "M1", "MZ"]
+        rd = ["D%d_%d" % (t, c) for c in range(N)] + ["OLD%d_0" % t, "M1", "ID"]
         before(q, rd, ["PA"])
-        g.tensor.matmul(T.PA[:, :], T.MZ[:, :], T.OLD[:, t * 1024:t * 1024 + 512], True, False)
+        g.tensor.matmul(T.PA[:, :], T.ID[:, :], T.OLD[:, t * 1024:t * 1024 + 512], True, False)
         g.tensor.matmul(T.PA[:, :], T.M1[:, :], dcol(t, 0, N), False, True).then_inc(T.sem.cp, 1)
         after(q, "cp", 1, rd, ["PA"])
 
     banks = ["PB", "PC"]
 
     def open2(q, t):
-        before(q, ["OLD%d_1" % t, "MZ"] if t else sw_res(1) + ["WA"], banks)
+        before(q, ["OLD%d_1" % t, "ID"] if t else sw_res(1) + ["WA"], banks)
         for k in range(2):
             a = t * 1024 + 512 + 256 * k
             if t:
-                g.tensor.matmul(T[banks[k]][:, 0:256], T.MZ[:, :], T.OLD[:, a:a + 256], True, False)
+                g.tensor.matmul(T[banks[k]][:, 0:256], T.ID[:, :], T.OLD[:, a:a + 256], True, False)
             else:
-                g.tensor.matmul(T[banks[k]][:, 0:256], T.WA[:, 15:143], T.SW[:, 16 + a:16 + a + 256], True, False)
+                g.tensor.matmul(T[banks[k]][:, 0:256], T.WA[:, 15:143], T.SW[:, Z + a:Z + a + 256], True, False)
 
     def close2(q, t):
         order = [me, me ^ 1] + [c for c in range(N) if c // 2 != me // 2]
@@ -432,15 +426,15 @@ def rank_program(g, core, T, topo):
                 after(q, "cp", 1, ["D%d_3" % t, "DL%d" % t, "M2"], [banks[c // 2]])
 
     def keep1(q, t):
-        copy(q, [], ["PA", "EW%d_0" % t], T.EW[:, 16 + 1024 * t:16 + 1024 * t + 512], T.PA[:, :])
+        copy(q, [], ["PA", "EW%d_0" % t], T.EW[:, Z + 1024 * t:Z + 1024 * t + 512], T.PA[:, :])
 
     def keep2(q, t, k):
-        b = 16 + 1024 * t + 512 + 256 * k
+        b = Z + 1024 * t + 512 + 256 * k
         copy(q, [], [banks[k], "EW%d_%d" % (t, k + 1)], T.EW[:, b:b + 256], T[banks[k]][:, 0:256])
 
     def final(q, k):
         a, b = CUTS[k], CUTS[k + 1]
-        op(q, ew_res(R) + ["PTR4", "fld"], ["OUT%d" % k],
+        op(q, ew_res(R) + ["PTR%d" % (R + a // 64), "fld"], ["OUT%d" % k],
            lambda: V.tensor_tensor(T.OUT[:, 16 * a:16 * b], T.EW[:, :].indirect(ptr(R, a, b)), T.FD[:, 16 * a:16 * b], A.add))
 
     def last(q, k, stage):
@@ -448,7 +442,7 @@ def rank_program(g, core, T, topo):
         bank, n = ("PD", "PS0")[k % 2], 16 * (b - a)
         got = T.OLD[:, 512 * (k % 2):512 * (k % 2) + n]
         if stage == 0:
-            gather(q, ew_res(R) + ["PTR4"], ["G%d" % k], got, T.EW[:, :], ptr(R, a, b))
+            gather(q, ew_res(R) + ["PTR%d" % (R + a // 64)], ["G%d" % k], got, T.EW[:, :], ptr(R, a, b))
         elif stage == 1:
             before(q, ["fld", "ID"], [bank])
             g.tensor.matmul(T[bank][:, 0:n], T.ID[:, :], T.FD[:, 16 * a:16 * b], True, False)
@@ -463,7 +457,7 @@ def rank_program(g, core, T, topo):
 
     steps = {"load": load, "own": own, "law": law, "species": species, "iota": iota, "rows_out": rows_out, "rows_in": rows_in, "fill": fill,
              "const": const, "mat": mat, "double": double, "zero": zero, "unreacted": unreacted, "xt": xt, "lo": lo, "narrow": narrow,
-             "scatter": scatter, "pgather": pgather, "first": first, "pwrap": pwrap, "pcast": pcast, "sgather": sgather, "prewrap": prewrap, "wrap": wrap,
+             "scatter": scatter, "pgather": pgather, "first": first, "pwrap": pwrap, "pcast": pcast, "sgather": sgather, "wrap": wrap,
              "wrap_u": wrap_u, "post": post, "exchange": exchange, "mine": mine, "join": join, "offsets": offsets, "new_u": new_u,
              "new_v": new_v, "raw": raw, "mask_u": mask_u, "send": send, "ogather": ogather, "sum1": sum1, "open2": open2,
              "close2": close2, "keep1": keep1, "keep2": keep2, "final": final, "last": last, "store": store}

from concourse.bass import DstId, RemoteDMATransfer
from concourse.mybir import AluOpType as A, ActivationFunctionType as F

N, P, R, Z = 4, 2048, 4, 128
BF, F32, I32, U16 = "bfloat16", "float32", "int32", "uint16"
SCRATCH = {
    "la32": ("sbuf", [128, 4, 32], I32), "lb32": ("sbuf", [128, 4, 32], I32),
    "L": ("sbuf", [128, 4, 64], U16),
    "FD": ("sbuf", [128, 2048], BF),
    "EW": ("sbuf", [128, 4224], BF),
    "SW": ("sbuf", [128, 3200], BF),
    "T2": ("sbuf", [128, 4096], BF),
    "LW": ("sbuf", [128, 4096], BF),
    "PW": ("sbuf", [128, 2048], BF),
    "XT": ("sbuf", [128, 4096], BF),
    "OLD": ("sbuf", [128, 4096], BF), "GS": ("sbuf", [128, 4096], BF), "GP": ("sbuf", [128, 4096], BF),
    "D": ("sbuf", [128, 2048], BF),
    "DL": ("sbuf", [128, 16, 128], BF),
    "RX": ("sbuf", [128, 16, 64], BF),
    "OFF": ("sbuf", [128, 256], U16), "PTR": ("sbuf", [128, 384], U16),
    "OUT": ("sbuf", [128, 2048], F32),
    "RW": ("sbuf", [128, 144], F32), "PK": ("sbuf", [128, 4], I32), "KM": ("sbuf", [128, 4], I32),
    "K15": ("sbuf", [128, 4], F32), "COL": ("sbuf", [128, 16], F32), "N0": ("sbuf", [128, 8], F32),
    "W0": ("sbuf", [128, 144], BF), "WA": ("sbuf", [128, 144], BF), "WP": ("sbuf", [128, 144], BF),
    "M1": ("sbuf", [128, 128], BF), "MZ": ("sbuf", [128, 128], BF), "M2": ("sbuf", [128, 128], BF), "ID": ("sbuf", [128, 128], BF),
    "R1": ("dram", [128, 256], BF), "RL": ("dram", [4, 128, 256], BF),
    "PS0": ("psum", [128, 512], F32), "PS1": ("psum", [128, 512], F32), "PU": ("psum", [128, 512], F32), "PP": ("psum", [128, 512], F32),
    "PA": ("psum", [128, 512], F32), "PB": ("psum", [128, 512], F32), "PC": ("psum", [128, 512], F32), "PD": ("psum", [128, 512], F32),
}
SEMAPHORES = (["cv", "cs", "cp", "cg", "sent0", "sent"] + ["at%d" % r for r in range(N)] + ["ax%d" % t for t in range(R)] + ["ad%d" % t for t in range(R)]
              + ["m%d" % k for k in range(36)])

PLAN = """
load y r1; load y la; load y lb; iota g PK; iota g RW; iota g K15; fill v 0 8; fill s 8 16; species y T2; const v KM; zero v 2 3;
const v KF; zero v 3 4; const v E; zero v 0 2; species y PW; fill y 16 32; const s N0; double s 0; double s 2; double s 4; double s 6;
narrow v 0; narrow v 1; first s 0; first s 1; double v 1; double v 3; mat v WA; double v 5; double v 7; scatter v 0 0 4; mat v ID; own y 16;
pgather v 1 2 4; rows_out g; xt g 1 0; rows_in y; wrap p 0; const s CWP; const s SW; const s EW; mat s WP; post s 0; mine p 0; exchange g 0; join p 0; offsets v 0;
xt g 1 1; lo y 1 0; lo y 1 1; xt g 2 0; xt g 2 1; pgather s 1 0 2; const s NE; new_u v 0; new_v s 0; pwrap p 1; pcast v 1;

sgather s 1 48 64; sgather s 1 0 32; scatter v 1 0 1; sgather v 1 32 48; wrap p 1; const s CW2; mat s M2; post s 1; law y 0 2 sent0; law y 2 4; raw s 0 0 4; lo y 2 0;
lo y 2 1; exchange g 1; mat y M2row; send g 0 0; send g 0 1; xt g 3 0; lo y 3 0; scatter v 1 1 4; pgather s 2 0 2; pgather v 2 2 4; mine p 1; join p 1;
offsets v 1; new_v s 1; raw v 1 0 4; send g 1 0; send g 1 1; xt g 3 1; lo y 3 1; pwrap p 2; pcast v 2; mat s M1; mask_u v 1;

sgather s 2 48 64; sgather s 2 0 32; scatter v 2 0 1; sgather v 2 32 48; open2 p 0; close2 p 0; keep2 s 0 0; keep2 s 0 1; wrap p 2; post s 2; mine p 2; ogather s 1 0;
ogather s 1 1; open2 p 1; scatter v 2 1 4; pgather v 3 2 4; pgather s 3 0 2; exchange g 2; load y fld AX2; unreacted y; join p 2; offsets v 2;
raw v 2 0 4; send g 2 0; new_v s 2; close2 p 1; keep2 s 1 0; pwrap p 3; pcast v 3; sum1 p 1; mask_u v 2;

sgather s 3 32 48; keep2 v 1 1; sgather v 3 48 64; wrap p 3; keep1 v 1; sgather s 3 0 32; post s 3; exchange g 3; scatter v 3 0 3;
ogather s 2 0; ogather s 2 1; sum1 p 2; keep1 s 2; send g 2 1; wrap_u p; join p 3; offsets v 3;

raw s 3 0; raw v 3 1; send g 3 0; open2 p 2; close2 p 2; scatter v 3 3 4; pwrap p 4; keep2 s 2 1; keep2 s 2 0; raw v 3 2; send g 3 1; raw s 3 3;
ogather s 3 0; ogather v 3 1; pcast v 4; sum1 p 3; keep1 v 3; open2 p 3; close2 p 3; pwrap p 5; keep2 s 3 1; keep2 v 3 0;
last s 2 0; final v 0; pcast v 5; store y 0 1; final v 1; store y 1 2; last s 5 0; last p 2 1; last p 5 1; last s 2 2; final v 3;
store y 2 4; last s 5 2; final v 4; store y 4 6
"""
ORDER = [tuple(int(w) if w.isdigit() else w for w in x.split()) for x in PLAN.split(";")]
CUTS = [0, 8, 36, 64, 88, 112, 128]


def rank_program(g, core, T, topo):
    me = T.rank_of(core)
    if me is None:
        return
    Q = {"v": g.vector, "s": g.scalar, "p": g.tensor, "g": g, "y": g.sync}
    own_sem = {"v": "cv", "s": "cs", "p": "cp", "g": "cg"}
    total, waited = {}, {}
    seen = {q: {} for q in Q}
    writer, readers = {}, {}
    ndma = [0]

    def need(q, tok):
        sem, val, known = tok
        if seen[q].get(sem, 0) < val:
            Q[q].wait_ge(T.sem[sem], val)
            waited[sem] = max(waited.get(sem, 0), val)
            seen[q][sem] = val
            for k, v in known.items():
                seen[q][k] = max(seen[q].get(k, 0), v)

    def before(q, rd, wr):
        toks = [writer[r] for r in rd + wr if r in writer] + [k for r in wr for k in readers.get(r, [])]
        for tok in sorted(toks, key=lambda k: -k[1]):
            need(q, tok)

    def after(q, sem, n, rd, wr):
        total[sem] = total.get(sem, 0) + n
        tok = (sem, total[sem], dict(seen[q]))
        for r in rd:
            readers.setdefault(r, []).append(tok)
        for r in wr:
            writer[r] = tok
            readers[r] = []

    def op(q, rd, wr, call):
        before(q, rd, wr)
        call().then_inc(T.sem[own_sem[q]], 1)
        after(q, own_sem[q], 1, rd, wr)

    def dma(q, rd, wr, out, in_):
        before(q, rd, wr)
        sem = "m%d" % ndma[0]
        ndma[0] += 1
        Q[q].dma_start(out, in_).then_inc(T.sem[sem], 16)
        after(q, sem, 16, rd, wr)

    others = [(me + d) % N for d in range(1, N)]
    ids = {}
    for q in others:
        rid, pid = topo.addr(T.cores[q])[:2]
        ids[q] = DstId(rid=rid, pnc=pid)
    eng = [e for e in topo.engines(T.cores[0], T.cores[1])
           if all(e in topo.engines(a, b) for a in T.cores for b in T.cores if a != b)]
    ne = len(eng)

    def bits(es):
        return sum(1 << e for e in es)

    def cast(rd, src, dst, arr, res, loc):
        before("g", rd, [res, loc])
        g.remote_dma_fused([RemoteDMATransfer(dst_ids=[ids[q] for q in others], dma_engine_mask=bits(eng), remote_sem=T.sem[arr],
                                              srcs=[src], dsts=[dst] * len(others))], local_sem=T.sem[loc])
        after("g", loc, ne, [], [loc] if loc != "sent" else [])
        total[arr] = ne * len(others)
        writer[res] = (arr, total[arr], {})

    def deal(r):
        far = sorted([(r + d) % N for d in range(1, N)], key=lambda q: topo.die(T.cores[q]) == topo.die(T.cores[r]))
        return [[(far[0], eng[:ne // 2]), (far[1], eng[ne // 2:])], [(far[2], eng)]]

    turn = [r for part in deal(me) for r, es in part] + [me]

    def dcol(t, a, b):
        return T.D[:, t * 512 + 128 * a:t * 512 + 128 * b] if t else T.EW[:, Z + 128 * a:Z + 128 * b]

    def send(q, t, k):
        part = deal(me)[k]
        before("g", ["D%d_%d" % (t, turn.index(r)) for r, es in part], ["DL%d" % t])
        g.remote_dma_fused([RemoteDMATransfer(dst_ids=[ids[r]], dma_engine_mask=bits(es), remote_sem=T.sem["ad%d" % t],
                                              src=dcol(t, r, r + 1), dst=T.DL[:, t * 4 + me])
                            for r, es in part], local_sem=T.sem.sent)
        after("g", "sent", ne, [], [])
        if k:
            total["ad%d" % t] = sum(len(es) for r in others for pt in deal(r) for x, es in pt if x == me)
            writer["DL%d" % t] = ("ad%d" % t, total["ad%d" % t], {})

    V, S = g.vector, g.scalar
    KF, E0, NE0, CWP, CW2 = 0, 1, 6, 8, 9

    def col(k):
        return T.COL[:, k:k + 1]

    def gather(q, rd, wr, out, win, off, scale=None):
        if q == "s":
            if scale is None:
                op(q, rd, wr, lambda: S.activation(out, win.indirect(off), F.Copy))
            else:
                op(q, rd, wr, lambda: S.activation(out, win.indirect(off), F.Copy, scale=scale))
        elif scale is None:
            op(q, rd, wr, lambda: V.tensor_copy(out, win.indirect(off)))
        else:
            op(q, rd, wr, lambda: V.tensor_scalar(out, win.indirect(off), scale, None, A.mult))

    def copy(q, rd, wr, out, in_, scale=None, bias=None):
        if q == "s":
            if bias is not None:
                op(q, rd, wr, lambda: S.activation(out, in_, F.Identity, bias=bias, scale=1.0 if scale is None else scale))
            elif scale is not None:
                op(q, rd, wr, lambda: S.activation(out, in_, F.Copy, scale=scale))
            else:
                op(q, rd, wr, lambda: S.activation(out, in_, F.Copy))
        elif bias is not None and scale is not None:
            op(q, rd, wr, lambda: V.tensor_scalar(out, in_, scale, bias, A.mult, A.add))
        elif bias is not None:
            op(q, rd, wr, lambda: V.tensor_scalar(out, in_, bias, None, A.add))
        elif scale is not None:
            op(q, rd, wr, lambda: V.tensor_scalar(out, in_, scale, None, A.mult))
        else:
            op(q, rd, wr, lambda: V.tensor_copy(out, in_))

    def wrap16(rd, bank, n, w, src, a, start=True, stop=True):
        before("p", rd + [w], [bank] if start else [])
        for s in range(16):
            ins = g.tensor.matmul(T[bank][:, 0:n], T[w][:, 15 - s:143 - s], T[src][:, a + s:a + 16 * n:16], start and s == 0, stop and s == 15)
        if stop:
            ins.then_inc(T.sem.cp, 1)
            after("p", "cp", 1, rd + [w], [bank])

    def members(t, a, b):
        return T.L[:, t, 16 * a:16 * b], sorted({a // 2, (b - 1) // 2})

    def ptr(t, a, b):
        return T.PTR[:, 64 * (t - 1) + a:64 * (t - 1) + b]

    def sw_res(t):
        return ["SW"] + ["SW%d_%d" % (k, c) for k in range(t) for c in range(5)]

    def ew_res(t):
        return ["EW"] + ["D0_%d" % c for c in range(N)] + ["EW%d_%d" % (k, c) for k in range(t) for c in range(3)]

    fill_res = ["T2f%d" % k for k in range(32)]
    t2_res = fill_res + ["T2_%d" % k for k in range(5)]
    row = dict([(me, 1)] + [(r, 2 + k) for k, r in enumerate(others)])
    lw_res = ["LW%d" % k for k in range(4)]

    def load(q, what, gate=None):
        before(q, [gate] if gate else [], [])
        if what == "r1":
            dma(q, [], ["R1"], T.R1[:, :], T.law[1:128:16, :])
        elif what == "la":
            dma(q, [], ["la32"], T.la32[:], T.la[:, :])
        elif what == "lb":
            dma(q, [], ["lb32"], T.lb32[:], T.lb[:, :])
        else:
            dma(q, [], ["fld"], T.FD[:, :], T.fld[:, :])

    def own(q, a, r0=0):
        for r in range(r0, 2):
            dma(q, fill_res[:a], ["T2_%d" % r], T.T2[r:128:16, 0:128 * a], T.law[r:128:16, 0:128 * a])

    def law(q, a, b, gate=None):
        before(q, [gate] if gate else [], [])
        dma(q, [], lw_res[a:b], T.LW[:, 1024 * a:1024 * b], T.law[:, 1024 * a:1024 * b])

    def species(q, where):
        if where == "PW":
            dma(q, ["PW%d" % k for k in range(4)], ["PW"], T.PW[0:128:16, :], T.fld[0:128:16, :])
        else:
            dma(q, fill_res[:16], ["T2_0"], T.T2[0:128:16, 0:P], T.fld[0:128:16, :])

    def iota(q, what):
        if what == "PK":
            op(q, [], ["PK"], lambda: g.iota(T.PK[:, 0:1], [[0, 1]], 0, 1))
        elif what == "RW":
            op(q, [], ["RW"], lambda: g.iota(T.RW[:, :], [[1, 144]], 0, 0, allow_small_or_imprecise_dtypes=True))
        else:
            op(q, [], ["K15"], lambda: g.iota(T.K15[:, 0:1], [[0, 1]], 15, 1, allow_small_or_imprecise_dtypes=True))

    def rows_out(q):
        cast(["R1"], T.R1[:, :], T.RL[me], "at%d" % me, "RL", "sent")
        del total["at%d" % me]
        for r in others:
            total["at%d" % r] = ne
            writer["RL%d" % r] = ("at%d" % r, ne, {})

    def rows_in(q):
        for r in others[::-1]:
            dma(q, ["RL%d" % r] + fill_res, ["T2_%d" % row[r]], T.T2[row[r]:128:16, :], T.RL[r])

    def fill(q, a, b):
        out = T.T2[:, 128 * a:128 * b]
        if q == "g":
            op(q, [], fill_res[a:b], lambda: g.iota(out, [[0, 128 * (b - a)]], 0, 0, allow_small_or_imprecise_dtypes=True))
        elif q == "v":
            op(q, [], fill_res[a:b], lambda: V.memset(out, 0.0))
        elif q == "y":
            dma(q, [], fill_res[a:b], out, T.law[:, 128 * a:128 * b])
        else:
            copy(q, fill_res[:b - a], fill_res[a:b], out, T.T2[:, 0:128 * (b - a)])

    def const(q, k):
        if k == "KM":
            op(q, ["PK"], ["KM"], lambda: V.tensor_scalar(T.KM[:, 0:1], T.PK[:, 0:1], 15, None, A.bitwise_and))
        elif k == "KF":
            copy(q, ["KM"], ["KF"], col(KF), T.KM[:, 0:1])
        elif k == "E":
            op(q, ["RW", "KF"], ["E"], lambda: V.tensor_scalar(T.COL[:, E0:E0 + 5], T.RW[:, 0:5], col(KF), None, A.is_equal))
        elif k == "N0":
            copy(q, ["RW", "E"], [k], T.N0[:, :], T.RW[:, 1:9], col(E0 + 1))
        elif k == "CWP":
            copy(q, ["E"], [k], col(CWP), col(E0 + 1), 128.0, col(E0))
        elif k == "NE":
            copy(q, ["E"], [k], T.COL[:, NE0:NE0 + 2], T.COL[:, E0:E0 + 2], -1.0, 1.0)
        elif k == "CW2":
            copy(q, ["E", "NE"], [k], col(CW2), col(NE0 + 1), -1.0, col(E0))
        else:
            copy(q, ["RW", "E"], [k], T[k][:, 0:Z], T.RW[:, 0:Z], col(E0))

    def mat(q, name):
        if name == "WA":
            op(q, ["RW", "KF", "K15"], [name], lambda: V.tensor_scalar(T.WA[:, :], T.RW[:, :], col(KF), T.K15[:, 0:1], A.add, A.is_equal))
        elif name == "ID":
            op(q, ["RW", "K15"], [name], lambda: V.tensor_scalar(T.ID[:, :], T.RW[:, 15:143], T.K15[:, 0:1], None, A.is_equal))
        elif name == "M2row":
            dma(q, ["WA"], ["M2"], T.M2[1:128:16, :], T.WA[1:128:16, 15:143])
        else:
            src, rd, c = {"WP": ("WA", "CWP", CWP), "M1": ("ID", "NE", NE0 + 1), "M2": ("ID", "CW2", CW2)}[name]
            copy(q, [src, rd], [name], T[name][:, :], T[src][:, :], col(c))

    def double(q, k):
        copy(q, ["RW", "E", "N0"], ["XT0_%d" % k], T.XT[:, 128 * k:128 * k + 128], T.RW[:, 0:128], col(E0), T.N0[:, k:k + 1])

    def zero(q, a, b):
        op(q, [], ["PW%d" % k for k in range(a, b)], lambda: V.memset(T.PW[:, 512 * a:512 * b], 0.0))

    def unreacted(q):
        dma(q, fill_res[:16], ["fld"], T.FD[0:128:16, :], T.T2[5:128:16, 0:P])

    def xt(q, t, h):
        a = t * 1024 + h * 512
        op(q, [], ["XT%d_%d" % (t, h)],
           lambda: g.iota(T.XT[:, a:a + 512], [[1, 4], [0, 128]], 1 + 8 * t + 4 * h, 0, allow_small_or_imprecise_dtypes=True))

    def lo(q, t, h):
        a = t * 1024 + h * 512
        dma(q, ["XT0_%d" % k for k in range(4)], ["XT%d_%d" % (t, h)], T.XT[0:128:16, a:a + 512], T.XT[0:128:16, 0:512])

    def narrow(q, h):
        copy(q, [("la32", "lb32")[h]], ["L%d" % h], T.L[:, :, 32 * h:32 * h + 32], (T.la32, T.lb32)[h][:])

    def scatter(q, t, a, b):
        off, hs = members(t, a, b)
        op(q, ["XT%d_%d" % (t, h) for h in (hs if t else range(2 * a, 2 * b))] + ["L%d" % h for h in hs], ["PW"],
           lambda: V.tensor_copy(T.PW[:, :].indirect(off), T.XT[:, t * 1024 + 256 * a:t * 1024 + 256 * b]))

    def gp_res(t, a=0, b=4):
        return ["GP%d_%d" % (t, k) for k in range(a, b)]

    def pgather(q, t, a, b):
        off, hs = members(t, a, b)
        gather(q, ["PW"] + ["L%d" % h for h in hs], gp_res(t, a, b), T.GP[:, t * 1024 + 256 * a:t * 1024 + 256 * b], T.PW[:, :], off)

    def first(q, h):
        gather(q, fill_res[:16] + ["T2_0", "L%d" % h], gp_res(0, 2 * h, 2 * h + 2), T.GP[:, h * 512:h * 512 + 512], T.T2[:, 0:P], members(0, 2 * h, 2 * h + 2)[0], None if h else 64.0)

    def pwrap(q, t):
        if t < R:
            wrap16(gp_res(t), "PP", 64, "WP", "GP", t * 1024)
        else:
            wrap16(["PW"], "PP" if t == R else "PS1", 64, "WP", "PW", 1024 * (t - R))

    def pcast(q, t):
        bank = "PP" if t <= R else "PS1"
        copy(q, [], [bank, "PTR%d" % t], ptr(t, 0, 64), T[bank][:, 0:64])

    def sgather(q, t, a, b):
        gather(q, sw_res(t) + ["PTR%d" % t], ["GS%d_%d" % (t, k) for k in range(a, b, 16)], T.GS[:, t * 1024 + 16 * a:t * 1024 + 16 * b], T.SW[:, 0:Z + 1024 * t],
               ptr(t, a, b), 64.0 if a < 32 else None)

    def wrap(q, t):
        if t == 0:
            wrap16(gp_res(0), "PS0", 64, "WA", "GP", 0)
        elif t < R - 1:
            wrap16(["GS%d_%d" % (t, k) for k in range(0, 64, 16)], "PS%d" % (t % 2), 64, "WA", "GS", t * 1024)
        else:
            wrap16(["GS3_32", "GS3_48"], "PS1", 32, "WA", "GS", t * 1024 + 512)

    def wrap_u(q):
        wrap16(["GS3_0", "GS3_16"], "PU", 32, "WA", "GS", 3 * 1024, stop=False)

    def post(q, t):
        a = 0 if t < R - 1 else 32
        bank = "PS%d" % (t % 2)
        copy(q, [], [bank, "RX%d" % t], T.RX[:, t * 4 + me, a:64], T[bank][:, 0:64 - a])

    def exchange(q, t):
        a = 0 if t < R - 1 else 32
        cast(["RX%d" % t], T.RX[:, t * 4 + me, a:64], T.RX[:, t * 4 + me, a:64], "ax%d" % t, "AX%d" % t, "sent0" if t == 0 else "sent")

    def mine(q, t):
        before(q, ["RX%d" % t, "ID"], ["PU"])
        g.tensor.matmul(T.PU[:, 0:64], T.ID[:, :], T.RX[:, t * 4 + me, :], True, False)

    def join(q, t):
        halves = 2 if t < R - 1 else 1
        rd = ["AX%d" % t, "RX%d" % t, "ID"]
        before(q, rd, [])
        for h in range(halves):
            a = 32 * (1 - h) + 8 * me
            ins = g.tensor.matmul(T.PU[:, 32 * h:32 * h + 32], T.ID[:, :], T.RX[:, t * 4:t * 4 + 4, a:a + 8], False, h == halves - 1)
        ins.then_inc(T.sem.cp, 1)
        after(q, "cp", 1, rd, ["PU"])

    def offsets(q, t):
        n = 64 if t < R - 1 else 32
        copy(q, [], ["PU", "OFF%d" % t], T.OFF[:, t * 64:t * 64 + n], T.PU[:, 0:n])

    def new_u(q, t):
        b = Z + 1024 * t
        gather(q, t2_res + ["OFF%d" % t, "E"], ["SW%d_4" % t], T.SW[:, b:b + 512], T.T2[:, :], T.OFF[:, t * 64:t * 64 + 32], col(E0))

    def new_v(q, t, a=0, b=N):
        for c in range(a, b):
            k = Z + 1024 * t + 512 + 128 * c
            gather(q, t2_res + ["OFF%d" % t, "E"], ["SW%d_%d" % (t, c)], T.SW[:, k:k + 128], T.T2[:, :],
                   T.OFF[:, t * 64 + 32 + 8 * c:t * 64 + 40 + 8 * c], col(E0 + row[c]))

    def raw(q, t, a, b=None):
        a, b = (a, b) if b else (turn[a], turn[a] + 1)
        gather(q, lw_res + ["OFF%d" % t, "NE"], ["D%d_%d" % (t, turn.index(c)) for c in range(a, b)], dcol(t, a, b), T.LW[:, :],
               T.OFF[:, t * 64 + 8 * a:t * 64 + 8 * b], None if t else col(NE0 + 1))

    def mask_u(q, t):
        b = Z + 1024 * t
        copy(q, ["D%d_%d" % (t, c) for c in range(N)] + ["E"], ["SW%d_4" % t], T.SW[:, b:b + 512], dcol(t, 0, N), col(E0))

    def ogather(q, t, h):
        gather(q, ew_res(t) + ["PTR%d" % t, "NE"], ["OLD%d_%d" % (t, h)], T.OLD[:, t * 1024 + h * 512:t * 1024 + h * 512 + 512],
               T.EW[:, 0:Z + 1024 * t], ptr(t, 32 * h, 32 * h + 32), col(NE0))

    def sum1(q, t):
        rd = ["D%d_%d" % (t, c) for c in range(N)] + ["OLD%d_0" % t, "M1", "ID"]
        before(q, rd, ["PA"])
        g.tensor.matmul(T.PA[:, :], T.ID[:, :], T.OLD[:, t * 1024:t * 1024 + 512], True, False)
        g.tensor.matmul(T.PA[:, :], T.M1[:, :], dcol(t, 0, N), False, True).then_inc(T.sem.cp, 1)
        after(q, "cp", 1, rd, ["PA"])

    banks = ["PB", "PC"]

    def open2(q, t):
        before(q, ["OLD%d_1" % t, "ID"] if t else sw_res(1) + ["WA"], banks)
        for k in range(2):
            a = t * 1024 + 512 + 256 * k
            if t:
                g.tensor.matmul(T[banks[k]][:, 0:256], T.ID[:, :], T.OLD[:, a:a + 256], True, False)
            else:
                g.tensor.matmul(T[banks[k]][:, 0:256], T.WA[:, 15:143], T.SW[:, Z + a:Z + a + 256], True, False)

    def close2(q, t):
        order = [me, me ^ 1] + [c for c in range(N) if c // 2 != me // 2]
        for i, c in enumerate(order):
            before(q, ["D%d_3" % t if c == me else "DL%d" % t, "M2"], [])
            ins = g.tensor.matmul(T[banks[c // 2]][:, 128 * (c % 2):128 * (c % 2) + 128], T.M2[:, :],
                                  dcol(t, c, c + 1) if c == me else T.DL[:, t * 4 + c], False, i % 2 == 1)
            if i % 2:
                ins.then_inc(T.sem.cp, 1)
                after(q, "cp", 1, ["D%d_3" % t, "DL%d" % t, "M2"], [banks[c // 2]])

    def keep1(q, t):
        copy(q, [], ["PA", "EW%d_0" % t], T.EW[:, Z + 1024 * t:Z + 1024 * t + 512], T.PA[:, :])

    def keep2(q, t, k):
        b = Z + 1024 * t + 512 + 256 * k
        copy(q, [], [banks[k], "EW%d_%d" % (t, k + 1)], T.EW[:, b:b + 256], T[banks[k]][:, 0:256])

    def final(q, k):
        a, b = CUTS[k], CUTS[k + 1]
        op(q, ew_res(R) + ["PTR%d" % (R + a // 64), "fld"], ["OUT%d" % k],
           lambda: V.tensor_tensor(T.OUT[:, 16 * a:16 * b], T.EW[:, :].indirect(ptr(R, a, b)), T.FD[:, 16 * a:16 * b], A.add))

    def last(q, k, stage):
        a, b = CUTS[k], CUTS[k + 1]
        bank, n = ("PD", "PS0")[k % 2], 16 * (b - a)
        got = T.OLD[:, 512 * (k % 2):512 * (k % 2) + n]
        if stage == 0:
            gather(q, ew_res(R) + ["PTR%d" % (R + a // 64)], ["G%d" % k], got, T.EW[:, :], ptr(R, a, b))
        elif stage == 1:
            before(q, ["fld", "ID"], [bank])
            g.tensor.matmul(T[bank][:, 0:n], T.ID[:, :], T.FD[:, 16 * a:16 * b], True, False)
            before(q, ["G%d" % k], [])
            g.tensor.matmul(T[bank][:, 0:n], T.ID[:, :], got, False, True).then_inc(T.sem.cp, 1)
            after(q, "cp", 1, ["fld", "ID", "G%d" % k], [bank])
        else:
            copy(q, [], [bank, "OUT%d" % k], T.OUT[:, 16 * a:16 * b], T[bank][:, 0:n])

    def store(q, a, b):
        dma(q, ["OUT%d" % k for k in range(a, b)], ["y%d" % a], T.y[:, 16 * CUTS[a]:16 * CUTS[b]], T.OUT[:, 16 * CUTS[a]:16 * CUTS[b]])

    steps = {"load": load, "own": own, "law": law, "species": species, "iota": iota, "rows_out": rows_out, "rows_in": rows_in, "fill": fill,
             "const": const, "mat": mat, "double": double, "zero": zero, "unreacted": unreacted, "xt": xt, "lo": lo, "narrow": narrow,
             "scatter": scatter, "pgather": pgather, "first": first, "pwrap": pwrap, "pcast": pcast, "sgather": sgather, "wrap": wrap,
             "wrap_u": wrap_u, "post": post, "exchange": exchange, "mine": mine, "join": join, "offsets": offsets, "new_u": new_u,
             "new_v": new_v, "raw": raw, "mask_u": mask_u, "send": send, "ogather": ogather, "sum1": sum1, "open2": open2,
             "close2": close2, "keep1": keep1, "keep2": keep2, "final": final, "last": last, "store": store}
    for task in ORDER:
        steps[task[0]](*task[1:])
    for sem in sorted(total):
        if waited.get(sem, 0) < total[sem]:
            g.wait_ge(T.sem[sem], total[sem])
